import numpy as np
import ml_dtypes


def mxq(x, axis, fmt="e4m3"):
    dtype, down = {"e4m3": (ml_dtypes.float8_e4m3fn, 7), "e5m2": (ml_dtypes.float8_e5m2, 14)}[fmt]
    v = np.moveaxis(np.asarray(x, np.float32).astype(ml_dtypes.bfloat16).astype(np.float64), axis, -1)
    blocks = v.reshape(v.shape[:-1] + (-1, 32))
    amax = np.abs(blocks).max(-1, keepdims=True)
    byte = np.maximum(np.where(amax > 0, np.frexp(amax)[1] - 1 + 127, 0) - down, 1)
    scale = np.exp2(byte - 127.0)
    codes = (blocks / scale).astype(np.float32).astype(dtype).astype(np.float64)
    return np.moveaxis((codes * scale).reshape(v.shape), -1, axis)


WIDE = False


def mx_kscale(k):
    if not WIDE:
        return np.ones(k)
    levels = np.array([10, -10, 5, -5, 0])
    if k % 512:
        return np.exp2(np.random.permutation(np.resize(levels, k // 32))).repeat(32)
    a = np.empty((k // 512, 16))
    for p in range(k // 512):
        a[p, :8] = np.random.permutation(np.resize(levels, 8))
        for g in range(8):
            far = levels[np.abs(levels - a[p, g]) >= 10]
            a[p, g + 8] = far[np.random.randint(len(far))]
    return np.exp2(a.ravel()).repeat(32)


def f64(x):
    return np.asarray(x).astype(np.float64)


def striped(idx):
    return np.tile(idx.reshape(-1, 16).T, (8, 1)).astype(np.uint16)


def unstriped(offs):
    return offs[:16].T.reshape(-1).astype(np.int64)


E2M1 = np.array([0.0, 0.5, 1.0, 1.5, 2.0, 3.0, 4.0, 6.0, -0.0, -0.5, -1.0, -1.5, -2.0, -3.0, -4.0, -6.0])


def pack_weight(w, fmt):
    k, n = w.shape
    w = f64(np.asarray(w, np.float32).astype(ml_dtypes.bfloat16)).reshape(k // 32, 32, n)
    amax = np.abs(w).max(1)
    if fmt == "e4m3":
        byte = np.frexp(amax)[1] - 1 + 127 - 7
    else:
        mant, ex = np.frexp(amax / 6.0)
        byte = np.where(mant > 0.5, ex, ex - 1) + 127
    byte = np.clip(np.where(amax > 0, byte, 1), 1, 254)
    scaled = (w * np.exp2(127.0 - byte)[:, None, :]).reshape(k, n).astype(np.float32)
    by_word = np.ascontiguousarray(scaled.reshape(k // 512, 128, 4, n).transpose(0, 1, 3, 2))
    if fmt == "e4m3":
        words = by_word.astype(ml_dtypes.float8_e4m3fn).view(np.uint8)
    else:
        c = by_word.astype(ml_dtypes.float4_e2m1fn).view(np.uint8) & 0xF
        words = (c[..., 0::2] | (c[..., 1::2] << 4)).reshape(k // 512, 128, 2 * n)
    return np.ascontiguousarray(words), np.ascontiguousarray(byte.astype(np.uint8).reshape(k // 512, 16, n))


def unpack_weight(words, scales, fmt):
    g, _, n = scales.shape
    words = np.ascontiguousarray(words).reshape(g, 128, n, -1)
    if fmt == "e4m3":
        vals = words.view(ml_dtypes.float8_e4m3fn).astype(np.float64)
    else:
        nib = np.empty((g, 128, n, 4), np.uint8)
        nib[..., 0::2] = words & 0xF
        nib[..., 1::2] = words >> 4
        vals = E2M1[nib]
    vals = vals * np.repeat(np.exp2(scales.astype(np.float64) - 127.0), 8, axis=1)[..., None]
    return vals.transpose(0, 1, 3, 2).reshape(g * 512, n)


def pack_table(v):
    words, scales = pack_weight(v, "e4m3")
    return np.concatenate([words.reshape(words.shape[0], -1), scales.reshape(scales.shape[0], -1)], axis=1)


def unpack_table(tab):
    g, t = tab.shape[0], tab.shape[1] // 528
    return unpack_weight(tab[:, :512 * t].reshape(g, 128, t, 4), tab[:, 512 * t:].reshape(g, 16, t), "e4m3")


def silu(v):
    return v / (1.0 + np.exp(-np.maximum(v, -700.0)))


K, M, T, S = 2048, 1024, 4096, 1024


def setup_inputs():
    n = np.random.standard_normal
    s = mx_kscale(K)[:, None]
    p_w4 = pack_weight(n((K, M)) / np.sqrt(K) / s, "e2m1")
    return {
        "tab": pack_table(n((K, T)) * s),
        "w4_words": p_w4[0],
        "w4_scales": p_w4[1],
        "w8": (n((K, M)) / np.sqrt(K) / s).astype(np.float32),
        "offs": striped(np.random.permutation(T)[:S]),
    }


def reference(tab, w4_words, w4_scales, w8, offs):
    tab_ = unpack_table(tab)[:, unstriped(offs)]
    w4_ = unpack_weight(w4_words, w4_scales, "e2m1")
    w8_ = mxq(f64(w8), 0, "e4m3")
    y = tab_.T @ w4_
    u = tab_.T @ w8_
    y = silu(y) * u
    return y

@@ -1,0 +1,272 @@
+from contextlib import ExitStack
+
+import concourse.mybir as mybir
+
+K, M, T, S = 2048, 1024, 4096, 1024
+FLOPS = 2 * 2 * K * M * S
+
+F32 = mybir.dt.float32
+BF16 = mybir.dt.bfloat16
+I32 = mybir.dt.int32
+U32 = mybir.dt.uint32
+U16 = mybir.dt.uint16
+U8 = mybir.dt.uint8
+FP8X4 = mybir.dt.float8_e4m3fn_x4
+FP4X4 = mybir.dt.float4_e2m1fn_x4
+SILU = mybir.ActivationFunctionType.Silu
+MULT = mybir.AluOpType.mult
+
+P = 128
+PASSES = K // 512
+HALF = 512
+TOKENS = S // P
+KIB = 1024
+TABLE_AT = [15 * KIB, 48 * KIB, 0, 17 * KIB]
+PICKED_SCALES_AT = 16 * KIB
+W4_LATE_AT = [48 * KIB, 49 * KIB]
+PLANES_LATE_AT = 53 * KIB
+RAW_AT = {
+    (0, None): 55 * KIB,
+    (1, None): 0,
+    (2, 0): 17 * KIB,
+    (3, 0): 25 * KIB,
+    (2, 1): 55 * KIB,
+    (3, 1): 63 * KIB,
+}
+SCALAR_COLUMNS = {(2, 0): 256, (3, 0): 256, (1, 1): 256, (2, 1): 384, (3, 1): 384}
+GATE_BYTES = 4 * HALF
+GROUPED_AT = {(2, 1): 0, (3, 1): 4 * GATE_BYTES}
+
+
+def tile_list_tabglu_tm_none_kernel(tc, tab, w4_words, w4_scales, w8, offs, out):
+    nc = tc.nc
+    words_bytes = 512 * T
+
+    with ExitStack() as ctx:
+        keep = ctx.enter_context(tc.tile_pool(name="keep", bufs=1))
+        shared = ctx.enter_context(tc.tile_pool(name="shared", bufs=1))
+        stage = ctx.enter_context(tc.tile_pool(name="stage", bufs=5))
+        outs = ctx.enter_context(tc.tile_pool(name="outs", bufs=6))
+        gating = ctx.enter_context(tc.tile_pool(name="gating", bufs=1))
+        psum = ctx.enter_context(tc.psum_pool(name="psum", bufs=8))
+
+        offsets = keep.tile([P, S // 16], U16, name="offsets")
+        nc.sync.dma_start(offsets[:], offs)
+
+        warm = keep.tile([P, 1], F32, name="warm")
+        nc.gpsimd.memset(warm[:], 0.0)
+        warm_out = keep.tile([P, 1], F32, name="warm_out")
+        nc.scalar.activation(warm_out[:], warm[:], SILU)
+
+        w4_codes = {}
+        w4_planes = {}
+
+        def load_w4(tile, a0, a1, h):
+            nc.sync.dma_start(
+                tile[:], w4_words[a0:a1, :, h * 2 * HALF : (h + 1) * 2 * HALF].rearrange("a p x -> p a x").bitcast(I32)
+            )
+            for a in range(a0, a1):
+                w4_codes[a, h] = tile[:, a - a0, :]
+
+        def load_planes(engine, tile, h):
+            for q in range(4):
+                engine.dma_start(
+                    tile[32 * q : 32 * q + 4, :, :],
+                    w4_scales[:, 4 * q : 4 * q + 4, h * HALF : (h + 1) * HALF].rearrange("a r n -> r a n").bitcast(I32),
+                )
+            for a in range(PASSES):
+                w4_planes[a, h] = tile[:, a, :].bitcast(U8)
+
+        table = {}
+
+        def load_table(a):
+            table[a] = shared.tile([P, T], I32, align_bytes=256, offset=TABLE_AT[a], name=f"table{a}")
+            nc.sync.dma_start(table[a][:], tab[a, 0:words_bytes].rearrange("(p x) -> p x", p=P).bitcast(I32))
+
+        load_table(0)
+        w4_first = keep.tile([P, PASSES - 1, HALF // 2], I32, align_bytes=256, name="w4_first")
+        load_w4(w4_first, 0, PASSES - 1, 0)
+        table_scales = keep.tile([P, T // 4], I32, align_bytes=256, name="table_scales")
+        nc.vector.memset(table_scales[:], 0)
+        for q in range(4):
+            nc.gpsimd.dma_start(
+                table_scales[32 * q : 32 * q + 16, :],
+                tab[:, words_bytes + 4 * q * T : words_bytes + (4 * q + 4) * T]
+                .rearrange("a (r t) -> a r t", r=4)
+                .bitcast(I32),
+            )
+        moved = keep.tile([P, (PASSES - 1) * S // 4], I32, align_bytes=256, name="moved")
+        nc.gpsimd.memset(moved[:], 0)
+        planes_first = keep.tile([P, PASSES, HALF // 4], I32, align_bytes=256, name="planes_first")
+        nc.vector.memset(planes_first[:], 0)
+        load_planes(nc.sync, planes_first, 0)
+        load_table(1)
+        picked = [keep.tile([P, S], U32, align_bytes=256, name=f"picked{a}") for a in range(PASSES)]
+
+        def gather_words(a, parts=1):
+            n = S // parts
+            for i in range(parts):
+                nc.vector.tensor_copy(
+                    picked[a][:, i * n : (i + 1) * n],
+                    table[a][:].bitcast(U32).indirect(offsets[:, i * n // 16 : (i + 1) * n // 16]),
+                )
+
+        gather_words(0)
+        picked_scales = shared.tile([P, S], U8, align_bytes=256, offset=PICKED_SCALES_AT, name="picked_scales")
+        nc.vector.tensor_copy(picked_scales[:], table_scales[:].bitcast(U8).indirect(offsets[:]))
+        for a in range(1, PASSES):
+            nc.scalar.dma_start(
+                moved[0:112, (a - 1) * S // 4 : a * S // 4], picked_scales[4 * a : 4 * a + 112, :].bitcast(I32)
+            )
+        load_table(2)
+        load_table(3)
+
+        moved_u8 = moved[:].bitcast(U8)
+
+        def token_operand(a, t):
+            cols = slice(t * P, (t + 1) * P)
+            codes = picked[a][:, cols].bitcast(FP8X4)
+            if a == 0:
+                return codes, picked_scales[:, cols]
+            return codes, moved_u8[:, (a - 1) * S + t * P : (a - 1) * S + (t + 1) * P]
+
+        def multiply(acc, a, t, rhs, rhs_scale):
+            codes, scales = token_operand(a, t)
+            nc.tensor.matmul_mx(
+                out=acc[:],
+                lhsT=codes,
+                lhsT_scale=scales,
+                rhs=rhs,
+                rhs_scale=rhs_scale,
+                start=(a == 0),
+                stop=(a == PASSES - 1),
+            )
+
+        def mm_w4(acc, a, t, h):
+            multiply(acc, a, t, w4_codes[a, h].bitcast(U8).bitcast(FP4X4), w4_planes[a, h])
+
+        w8_codes = {}
+
+        def mm_w8(acc, a, t, h):
+            codes, scales = w8_codes[a, h]
+            multiply(acc, a, t, codes[:].bitcast(FP8X4), scales[:])
+
+        raws = {}
+
+        def load_w8(a, half):
+            if half is None:
+                cols, key = slice(0, M), f"raw{a}"
+            else:
+                cols, key = slice(half * HALF, (half + 1) * HALF), f"raw{a}{half}"
+            width = cols.stop - cols.start
+            raw = shared.tile([P, 4, width], F32, align_bytes=256, offset=RAW_AT[a, half], name=key)
+            nc.sync.dma_start(raw[:], w8[512 * a : 512 * (a + 1), cols].rearrange("(p j) n -> p j n", j=4))
+            for h in range(2) if half is None else [half]:
+                raws[a, h] = raw[:, :, h * HALF : (h + 1) * HALF] if half is None else raw[:]
+
+        def quantize_w8(a, h):
+            cut = SCALAR_COLUMNS.get((a, h), 0)
+            if (a, h) in GROUPED_AT:
+                grouped = gating.tile(
+                    [P, HALF, 4], BF16, align_bytes=256, offset=GROUPED_AT[a, h], name=f"grouped{a}{h}"
+                )
+            else:
+                grouped = stage.tile([P, HALF, 4], BF16, align_bytes=256, name="grouped")
+            dst = grouped[:].rearrange("p (c i) t -> p c t i", i=4)
+            src = raws[a, h].rearrange("p t (c i) -> p c t i", i=4)
+            if cut:
+                nc.scalar.copy(dst[:, : cut // 4], src[:, : cut // 4])
+            nc.vector.tensor_copy(dst[:, cut // 4 :], src[:, cut // 4 :])
+            codes = keep.tile([P, HALF], U32, align_bytes=256, name=f"w8_codes{a}{h}")
+            scales = keep.tile([P, HALF], U8, align_bytes=256, name=f"w8_scales{a}{h}")
+            nc.vector.quantize_mx(
+                out=codes[:].bitcast(FP8X4), scales=scales[:], in_=grouped[:].rearrange("p n t -> p (n t)")
+            )
+            w8_codes[a, h] = (codes, scales)
+
+        gates = {}
+
+        def gate(acc, t, h):
+            g = gating.tile([P, HALF], F32, align_bytes=256, offset=GATE_BYTES * (TOKENS * h + t), name=f"gate{t}{h}")
+            nc.scalar.activation(g[:], acc[:], SILU)
+            gates[t, h] = g
+
+        def finish(acc, t, h):
+            mm_w8(acc, PASSES - 1, t, h)
+            res = outs.tile([P, HALF], F32, name="res")
+            nc.vector.tensor_tensor(res[:], acc[:], gates[t, h][:], MULT)
+            nc.sync.dma_start(out[t * P : (t + 1) * P, h * HALF : (h + 1) * HALF], res[:])
+
+        accs = [psum.tile([P, HALF], F32, name="acc") for t in range(TOKENS)]
+        for a in range(PASSES):
+            if a > 0:
+                gather_words(a, 2 if a == PASSES - 1 else 1)
+            for t in range(TOKENS):
+                mm_w4(accs[t], a, t, 0)
+            if a == 1:
+                w4_late0 = shared.tile([P, 1, HALF // 2], I32, align_bytes=256, offset=W4_LATE_AT[0], name="w4_late0")
+                load_w4(w4_late0, 3, 4, 0)
+                w4_late1 = shared.tile([P, PASSES, HALF // 2], I32, align_bytes=256, offset=W4_LATE_AT[1], name="w4_late1")
+                load_w4(w4_late1, 0, 4, 1)
+                planes_late = shared.tile(
+                    [P, PASSES, HALF // 4], I32, align_bytes=256, offset=PLANES_LATE_AT, name="planes_late"
+                )
+                nc.vector.memset(planes_late[:], 0)
+                load_planes(nc.sync, planes_late, 1)
+                load_w8(0, None)
+            if a == 2:
+                load_w8(1, None)
+            if a == 3:
+                load_w8(2, 0)
+                load_w8(3, 0)
+        for t in range(TOKENS):
+            gate(accs[t], t, 0)
+
+        for t in range(TOKENS):
+            if t == 3:
+                quantize_w8(0, 0)
+                quantize_w8(0, 1)
+                load_w8(2, 1)
+                load_w8(3, 1)
+            if t == 7:
+                quantize_w8(1, 0)
+            acc = psum.tile([P, HALF], F32, name="acc")
+            for a in range(PASSES):
+                mm_w4(acc, a, t, 1)
+            gate(acc, t, 1)
+
+        accs = [psum.tile([P, HALF], F32, name="acc") for t in range(TOKENS)]
+        for a in range(2):
+            for t in range(TOKENS):
+                mm_w8(accs[t], a, t, 0)
+        quantize_w8(2, 0)
+        quantize_w8(3, 0)
+        quantize_w8(1, 1)
+        for t in range(TOKENS):
+            mm_w8(accs[t], 2, t, 0)
+            finish(accs[t], t, 0)
+            if t == 2:
+                quantize_w8(2, 1)
+            if t == 5:
+                quantize_w8(3, 1)
+
+        waiting = []
+        for t in range(TOKENS - 1):
+            acc = psum.tile([P, HALF], F32, name="acc")
+            for a in range(PASSES - 1):
+                mm_w8(acc, a, t, 1)
+            waiting.append((acc, t))
+            if t >= 2:
+                while waiting:
+                    finish(*waiting.pop(0), 1)
+        t = TOKENS - 1
+        n = HALF // 2
+        for part in range(2):
+            acc = psum.tile([P, n], F32, name="acc")
+            cols = slice(part * n, (part + 1) * n)
+            for a in range(PASSES):
+                codes, scales = w8_codes[a, 1]
+                multiply(acc, a, t, codes[:, cols].bitcast(FP8X4), scales[:, cols])
+            res = outs.tile([P, n], F32, name="res")
+            nc.vector.tensor_tensor(res[:], acc[:], gates[t, 1][:, cols], MULT)
+            nc.sync.dma_start(out[t * P : (t + 1) * P, HALF + part * n : HALF + (part + 1) * n], res[:])

@@ -21,21 +21,10 @@ PASSES = K // 512
 HALF = 512
 TOKENS = S // P
 KIB = 1024
-TABLE_AT = [15 * KIB, 48 * KIB, 0, 17 * KIB]
-PICKED_SCALES_AT = 16 * KIB
-W4_LATE_AT = [48 * KIB, 49 * KIB]
-PLANES_LATE_AT = 53 * KIB
-RAW_AT = {
-    (0, None): 55 * KIB,
-    (1, None): 0,
-    (2, 0): 17 * KIB,
-    (3, 0): 25 * KIB,
-    (2, 1): 55 * KIB,
-    (3, 1): 63 * KIB,
-}
-SCALAR_COLUMNS = {(2, 0): 256, (3, 0): 256, (1, 1): 256, (2, 1): 384, (3, 1): 384}
-GATE_BYTES = 4 * HALF
-GROUPED_AT = {(2, 1): 0, (3, 1): 4 * GATE_BYTES}
+TABLE_BYTES = 4 * T
+RAW_BYTES = 4 * 4 * HALF
+SCALAR_COLUMNS = 384
+AHEAD = 3
 
 
 def tile_list_tabglu_tm_none_kernel(tc, tab, w4_words, w4_scales, w8, offs, out):
@@ -45,21 +34,19 @@ def tile_list_tabglu_tm_none_kernel(tc, tab, w4_words, w4_scales, w8, offs, out)
     with ExitStack() as ctx:
         keep = ctx.enter_context(tc.tile_pool(name="keep", bufs=1))
         shared = ctx.enter_context(tc.tile_pool(name="shared", bufs=1))
-        stage = ctx.enter_context(tc.tile_pool(name="stage", bufs=5))
-        outs = ctx.enter_context(tc.tile_pool(name="outs", bufs=6))
-        gating = ctx.enter_context(tc.tile_pool(name="gating", bufs=1))
+        stage = ctx.enter_context(tc.tile_pool(name="stage", bufs=4))
         psum = ctx.enter_context(tc.psum_pool(name="psum", bufs=8))
 
         offsets = keep.tile([P, S // 16], U16, name="offsets")
         nc.sync.dma_start(offsets[:], offs)
 
-        warm = keep.tile([P, 1], F32, name="warm")
-        nc.gpsimd.memset(warm[:], 0.0)
-        warm_out = keep.tile([P, 1], F32, name="warm_out")
-        nc.scalar.activation(warm_out[:], warm[:], SILU)
+        table = {}
+
+        def load_table(a, at):
+            table[a] = shared.tile([P, T], I32, align_bytes=256, offset=at, name=f"table{a}")
+            nc.sync.dma_start(table[a][:], tab[a, 0:words_bytes].rearrange("(p x) -> p x", p=P).bitcast(I32))
 
         w4_codes = {}
-        w4_planes = {}
 
         def load_w4(tile, a0, a1, h):
             nc.sync.dma_start(
@@ -68,25 +55,8 @@ def tile_list_tabglu_tm_none_kernel(tc, tab, w4_words, w4_scales, w8, offs, out)
             for a in range(a0, a1):
                 w4_codes[a, h] = tile[:, a - a0, :]
 
-        def load_planes(engine, tile, h):
-            for q in range(4):
-                engine.dma_start(
-                    tile[32 * q : 32 * q + 4, :, :],
-                    w4_scales[:, 4 * q : 4 * q + 4, h * HALF : (h + 1) * HALF].rearrange("a r n -> r a n").bitcast(I32),
-                )
-            for a in range(PASSES):
-                w4_planes[a, h] = tile[:, a, :].bitcast(U8)
-
-        table = {}
-
-        def load_table(a):
-            table[a] = shared.tile([P, T], I32, align_bytes=256, offset=TABLE_AT[a], name=f"table{a}")
-            nc.sync.dma_start(table[a][:], tab[a, 0:words_bytes].rearrange("(p x) -> p x", p=P).bitcast(I32))
-
-        load_table(0)
-        w4_first = keep.tile([P, PASSES - 1, HALF // 2], I32, align_bytes=256, name="w4_first")
-        load_w4(w4_first, 0, PASSES - 1, 0)
-        table_scales = keep.tile([P, T // 4], I32, align_bytes=256, name="table_scales")
+        load_table(0, 0)
+        table_scales = shared.tile([P, T // 4], I32, align_bytes=256, offset=5 * TABLE_BYTES, name="table_scales")
         nc.vector.memset(table_scales[:], 0)
         for q in range(4):
             nc.gpsimd.dma_start(
@@ -95,12 +65,28 @@ def tile_list_tabglu_tm_none_kernel(tc, tab, w4_words, w4_scales, w8, offs, out)
                 .rearrange("a (r t) -> a r t", r=4)
                 .bitcast(I32),
             )
+        planes = keep.tile([P, PASSES, M // 4], I32, align_bytes=256, name="planes")
+        nc.vector.memset(planes[:], 0)
+        for q in range(4):
+            nc.gpsimd.dma_start(
+                planes[32 * q : 32 * q + 4, :, :],
+                w4_scales[:, 4 * q : 4 * q + 4, :].rearrange("a r n -> r a n").bitcast(I32),
+            )
+        planes_u8 = planes[:].rearrange("p a n -> p (a n)").bitcast(U8)
         moved = keep.tile([P, (PASSES - 1) * S // 4], I32, align_bytes=256, name="moved")
-        nc.gpsimd.memset(moved[:], 0)
-        planes_first = keep.tile([P, PASSES, HALF // 4], I32, align_bytes=256, name="planes_first")
-        nc.vector.memset(planes_first[:], 0)
-        load_planes(nc.sync, planes_first, 0)
-        load_table(1)
+        nc.vector.memset(moved[:], 0)
+
+        warm = keep.tile([P, 1], F32, name="warm")
+        nc.vector.memset(warm[:], 0.0)
+        warm_out = keep.tile([P, 1], F32, name="warm_out")
+        nc.scalar.activation(warm_out[:], warm[:], SILU)
+
+        load_table(1, TABLE_BYTES)
+        w4_first = keep.tile([P, PASSES - 1, HALF // 2], I32, align_bytes=256, name="w4_first")
+        load_w4(w4_first, 0, PASSES - 1, 0)
+        load_table(2, 2 * TABLE_BYTES)
+        load_table(3, 3 * TABLE_BYTES)
+
         picked = [keep.tile([P, S], U32, align_bytes=256, name=f"picked{a}") for a in range(PASSES)]
 
         def gather_words(a, parts=1):
@@ -111,30 +97,23 @@ def tile_list_tabglu_tm_none_kernel(tc, tab, w4_words, w4_scales, w8, offs, out)
                     table[a][:].bitcast(U32).indirect(offsets[:, i * n // 16 : (i + 1) * n // 16]),
                 )
 
-        gather_words(0)
-        picked_scales = shared.tile([P, S], U8, align_bytes=256, offset=PICKED_SCALES_AT, name="picked_scales")
+        picked_scales = keep.tile([P, S], U8, align_bytes=256, name="picked_scales")
         nc.vector.tensor_copy(picked_scales[:], table_scales[:].bitcast(U8).indirect(offsets[:]))
         for a in range(1, PASSES):
             nc.scalar.dma_start(
                 moved[0:112, (a - 1) * S // 4 : a * S // 4], picked_scales[4 * a : 4 * a + 112, :].bitcast(I32)
             )
-        load_table(2)
-        load_table(3)
-
         moved_u8 = moved[:].bitcast(U8)
 
-        def token_operand(a, t):
-            cols = slice(t * P, (t + 1) * P)
-            codes = picked[a][:, cols].bitcast(FP8X4)
-            if a == 0:
-                return codes, picked_scales[:, cols]
-            return codes, moved_u8[:, (a - 1) * S + t * P : (a - 1) * S + (t + 1) * P]
-
         def multiply(acc, a, t, rhs, rhs_scale):
-            codes, scales = token_operand(a, t)
+            cols = slice(t * P, (t + 1) * P)
+            if a == 0:
+                scales = picked_scales[:, cols]
+            else:
+                scales = moved_u8[:, (a - 1) * S + t * P : (a - 1) * S + (t + 1) * P]
             nc.tensor.matmul_mx(
                 out=acc[:],
-                lhsT=codes,
+                lhsT=picked[a][:, cols].bitcast(FP8X4),
                 lhsT_scale=scales,
                 rhs=rhs,
                 rhs_scale=rhs_scale,
@@ -143,37 +122,31 @@ def tile_list_tabglu_tm_none_kernel(tc, tab, w4_words, w4_scales, w8, offs, out)
             )
 
         def mm_w4(acc, a, t, h):
-            multiply(acc, a, t, w4_codes[a, h].bitcast(U8).bitcast(FP4X4), w4_planes[a, h])
+            at = a * M + h * HALF
+            multiply(acc, a, t, w4_codes[a, h].bitcast(U8).bitcast(FP4X4), planes_u8[:, at : at + HALF])
 
         w8_codes = {}
 
-        def mm_w8(acc, a, t, h):
+        def mm_w8(acc, a, t, h, cols=slice(0, HALF)):
             codes, scales = w8_codes[a, h]
-            multiply(acc, a, t, codes[:].bitcast(FP8X4), scales[:])
+            multiply(acc, a, t, codes[:, cols].bitcast(FP8X4), scales[:, cols])
 
         raws = {}
 
-        def load_w8(a, half):
-            if half is None:
-                cols, key = slice(0, M), f"raw{a}"
-            else:
-                cols, key = slice(half * HALF, (half + 1) * HALF), f"raw{a}{half}"
-            width = cols.stop - cols.start
-            raw = shared.tile([P, 4, width], F32, align_bytes=256, offset=RAW_AT[a, half], name=key)
-            nc.sync.dma_start(raw[:], w8[512 * a : 512 * (a + 1), cols].rearrange("(p j) n -> p j n", j=4))
-            for h in range(2) if half is None else [half]:
-                raws[a, h] = raw[:, :, h * HALF : (h + 1) * HALF] if half is None else raw[:]
+        def load_w8(a, h):
+            raw = shared.tile(
+                [P, 4, HALF], F32, align_bytes=256, offset=(PASSES * h + a) * RAW_BYTES, name=f"raw{a}{h}"
+            )
+            nc.sync.dma_start(
+                raw[:], w8[512 * a : 512 * (a + 1), h * HALF : (h + 1) * HALF].rearrange("(p j) n -> p j n", j=4)
+            )
+            raws[a, h] = raw
 
         def quantize_w8(a, h):
-            cut = SCALAR_COLUMNS.get((a, h), 0)
-            if (a, h) in GROUPED_AT:
-                grouped = gating.tile(
-                    [P, HALF, 4], BF16, align_bytes=256, offset=GROUPED_AT[a, h], name=f"grouped{a}{h}"
-                )
-            else:
-                grouped = stage.tile([P, HALF, 4], BF16, align_bytes=256, name="grouped")
+            cut = SCALAR_COLUMNS if h == 1 else 0
+            grouped = stage.tile([P, HALF, 4], BF16, align_bytes=256, name="grouped")
             dst = grouped[:].rearrange("p (c i) t -> p c t i", i=4)
-            src = raws[a, h].rearrange("p t (c i) -> p c t i", i=4)
+            src = raws[a, h][:].rearrange("p t (c i) -> p c t i", i=4)
             if cut:
                 nc.scalar.copy(dst[:, : cut // 4], src[:, : cut // 4])
             nc.vector.tensor_copy(dst[:, cut // 4 :], src[:, cut // 4 :])
@@ -187,86 +160,58 @@ def tile_list_tabglu_tm_none_kernel(tc, tab, w4_words, w4_scales, w8, offs, out)
         gates = {}
 
         def gate(acc, t, h):
-            g = gating.tile([P, HALF], F32, align_bytes=256, offset=GATE_BYTES * (TOKENS * h + t), name=f"gate{t}{h}")
+            g = keep.tile([P, HALF], F32, align_bytes=256, name=f"gate{t}{h}")
             nc.scalar.activation(g[:], acc[:], SILU)
             gates[t, h] = g
 
-        def finish(acc, t, h):
-            mm_w8(acc, PASSES - 1, t, h)
-            res = outs.tile([P, HALF], F32, name="res")
-            nc.vector.tensor_tensor(res[:], acc[:], gates[t, h][:], MULT)
-            nc.sync.dma_start(out[t * P : (t + 1) * P, h * HALF : (h + 1) * HALF], res[:])
+        def finish(acc, t, h, cols=slice(0, HALF)):
+            res = keep.tile([P, cols.stop - cols.start], F32, name=f"res{t}{h}{cols.start}")
+            nc.vector.tensor_tensor(res[:], acc[:], gates[t, h][:, cols], MULT)
+            nc.sync.dma_start(out[t * P : (t + 1) * P, h * HALF + cols.start : h * HALF + cols.stop], res[:])
 
         accs = [psum.tile([P, HALF], F32, name="acc") for t in range(TOKENS)]
         for a in range(PASSES):
-            if a > 0:
-                gather_words(a, 2 if a == PASSES - 1 else 1)
+            gather_words(a, 2 if a == PASSES - 1 else 1)
+            if a == 0:
+                w4_late = shared.tile(
+                    [P, PASSES + 1, HALF // 2], I32, align_bytes=256, offset=5 * TABLE_BYTES, name="w4_late"
+                )
+                load_w4(w4_late[:, 0:1], 3, 4, 0)
+                load_w4(w4_late[:, 1:], 0, 4, 1)
+            load_w8(2 * a % PASSES, a // 2)
+            load_w8(2 * a % PASSES + 1, a // 2)
             for t in range(TOKENS):
                 mm_w4(accs[t], a, t, 0)
-            if a == 1:
-                w4_late0 = shared.tile([P, 1, HALF // 2], I32, align_bytes=256, offset=W4_LATE_AT[0], name="w4_late0")
-                load_w4(w4_late0, 3, 4, 0)
-                w4_late1 = shared.tile([P, PASSES, HALF // 2], I32, align_bytes=256, offset=W4_LATE_AT[1], name="w4_late1")
-                load_w4(w4_late1, 0, 4, 1)
-                planes_late = shared.tile(
-                    [P, PASSES, HALF // 4], I32, align_bytes=256, offset=PLANES_LATE_AT, name="planes_late"
-                )
-                nc.vector.memset(planes_late[:], 0)
-                load_planes(nc.sync, planes_late, 1)
-                load_w8(0, None)
-            if a == 2:
-                load_w8(1, None)
-            if a == 3:
-                load_w8(2, 0)
-                load_w8(3, 0)
         for t in range(TOKENS):
             gate(accs[t], t, 0)
 
         for t in range(TOKENS):
-            if t == 3:
-                quantize_w8(0, 0)
-                quantize_w8(0, 1)
-                load_w8(2, 1)
-                load_w8(3, 1)
-            if t == 7:
-                quantize_w8(1, 0)
+            if t % 2 == 1:
+                quantize_w8(t // 2, 0)
             acc = psum.tile([P, HALF], F32, name="acc")
             for a in range(PASSES):
                 mm_w4(acc, a, t, 1)
             gate(acc, t, 1)
 
-        accs = [psum.tile([P, HALF], F32, name="acc") for t in range(TOKENS)]
-        for a in range(2):
-            for t in range(TOKENS):
-                mm_w8(accs[t], a, t, 0)
-        quantize_w8(2, 0)
-        quantize_w8(3, 0)
-        quantize_w8(1, 1)
-        for t in range(TOKENS):
-            mm_w8(accs[t], 2, t, 0)
-            finish(accs[t], t, 0)
-            if t == 2:
-                quantize_w8(2, 1)
-            if t == 5:
-                quantize_w8(3, 1)
-
-        waiting = []
-        for t in range(TOKENS - 1):
-            acc = psum.tile([P, HALF], F32, name="acc")
-            for a in range(PASSES - 1):
-                mm_w8(acc, a, t, 1)
-            waiting.append((acc, t))
-            if t >= 2:
-                while waiting:
-                    finish(*waiting.pop(0), 1)
+        for h in range(2):
+            waiting = []
+            for t in range(TOKENS - h):
+                acc = psum.tile([P, HALF], F32, name="acc")
+                for a in range(PASSES - 1):
+                    mm_w8(acc, a, t, h)
+                waiting.append((acc, t))
+                if t >= AHEAD - 1:
+                    while waiting:
+                        acc, tw = waiting.pop(0)
+                        mm_w8(acc, PASSES - 1, tw, h)
+                        finish(acc, tw, h)
+                if h == 0 and t % 2 == 1:
+                    quantize_w8(t // 2, 1)
         t = TOKENS - 1
         n = HALF // 2
         for part in range(2):
             acc = psum.tile([P, n], F32, name="acc")
             cols = slice(part * n, (part + 1) * n)
             for a in range(PASSES):
-                codes, scales = w8_codes[a, 1]
-                multiply(acc, a, t, codes[:, cols].bitcast(FP8X4), scales[:, cols])
-            res = outs.tile([P, n], F32, name="res")
-            nc.vector.tensor_tensor(res[:], acc[:], gates[t, 1][:, cols], MULT)
-            nc.sync.dma_start(out[t * P : (t + 1) * P, HALF + part * n : HALF + (part + 1) * n], res[:])
+                mm_w8(acc, a, t, 1, cols)
+            finish(acc, t, 1, cols)

@@ -56,7 +56,7 @@ def tile_list_tabglu_tm_none_kernel(tc, tab, w4_words, w4_scales, w8, offs, out)
                 w4_codes[a, h] = tile[:, a - a0, :]
 
         load_table(0, 0)
-        table_scales = shared.tile([P, T // 4], I32, align_bytes=256, offset=5 * TABLE_BYTES, name="table_scales")
+        table_scales = keep.tile([P, T // 4], I32, align_bytes=256, name="table_scales")
         nc.vector.memset(table_scales[:], 0)
         for q in range(4):
             nc.gpsimd.dma_start(
@@ -82,10 +82,12 @@ def tile_list_tabglu_tm_none_kernel(tc, tab, w4_words, w4_scales, w8, offs, out)
         nc.scalar.activation(warm_out[:], warm[:], SILU)
 
         load_table(1, TABLE_BYTES)
-        w4_first = keep.tile([P, PASSES - 1, HALF // 2], I32, align_bytes=256, name="w4_first")
-        load_w4(w4_first, 0, PASSES - 1, 0)
+        w4_first = keep.tile([P, PASSES, HALF // 2], I32, align_bytes=256, name="w4_first")
+        load_w4(w4_first, 0, PASSES, 0)
         load_table(2, 2 * TABLE_BYTES)
         load_table(3, 3 * TABLE_BYTES)
+        w4_late = keep.tile([P, PASSES, HALF // 2], I32, align_bytes=256, name="w4_late")
+        load_w4(w4_late, 0, PASSES, 1)
 
         picked = [keep.tile([P, S], U32, align_bytes=256, name=f"picked{a}") for a in range(PASSES)]
 
@@ -172,12 +174,6 @@ def tile_list_tabglu_tm_none_kernel(tc, tab, w4_words, w4_scales, w8, offs, out)
         accs = [psum.tile([P, HALF], F32, name="acc") for t in range(TOKENS)]
         for a in range(PASSES):
             gather_words(a, 2 if a == PASSES - 1 else 1)
-            if a == 0:
-                w4_late = shared.tile(
-                    [P, PASSES + 1, HALF // 2], I32, align_bytes=256, offset=5 * TABLE_BYTES, name="w4_late"
-                )
-                load_w4(w4_late[:, 0:1], 3, 4, 0)
-                load_w4(w4_late[:, 1:], 0, 4, 1)
             load_w8(2 * a % PASSES, a // 2)
             load_w8(2 * a % PASSES + 1, a // 2)
             for t in range(TOKENS):

@@ -44,7 +44,9 @@ def tile_list_tabglu_tm_none_kernel(tc, tab, w4_words, w4_scales, w8, offs, out)
 
         def load_table(a, at):
             table[a] = shared.tile([P, T], I32, align_bytes=256, offset=at, name=f"table{a}")
-            nc.sync.dma_start(table[a][:], tab[a, 0:words_bytes].rearrange("(p x) -> p x", p=P).bitcast(I32))
+            nc.sync.dma_start(
+                table[a][:], tab[a, 0:words_bytes].rearrange("(p x) -> p x", p=P).bitcast(I32), max_dma_last_dim=4 * KIB
+            )
 
         w4_codes = {}
 

@@ -24,7 +24,7 @@ KIB = 1024
 TABLE_BYTES = 4 * T
 RAW_BYTES = 4 * 4 * HALF
 SCALAR_COLUMNS = 384
-AHEAD = 3
+AHEAD = 4
 
 
 def tile_list_tabglu_tm_none_kernel(tc, tab, w4_words, w4_scales, w8, offs, out):
@@ -35,7 +35,7 @@ def tile_list_tabglu_tm_none_kernel(tc, tab, w4_words, w4_scales, w8, offs, out)
         keep = ctx.enter_context(tc.tile_pool(name="keep", bufs=1))
         shared = ctx.enter_context(tc.tile_pool(name="shared", bufs=1))
         stage = ctx.enter_context(tc.tile_pool(name="stage", bufs=4))
-        psum = ctx.enter_context(tc.psum_pool(name="psum", bufs=8))
+        psum = ctx.enter_context(tc.psum_pool(name="psum", bufs=1))
 
         offsets = keep.tile([P, S // 16], U16, name="offsets")
         nc.sync.dma_start(offsets[:], offs)
@@ -58,7 +58,7 @@ def tile_list_tabglu_tm_none_kernel(tc, tab, w4_words, w4_scales, w8, offs, out)
                 w4_codes[a, h] = tile[:, a - a0, :]
 
         load_table(0, 0)
-        table_scales = keep.tile([P, T // 4], I32, align_bytes=256, name="table_scales")
+        table_scales = shared.tile([P, T // 4], I32, align_bytes=256, offset=4 * TABLE_BYTES, name="table_scales")
         nc.vector.memset(table_scales[:], 0)
         for q in range(4):
             nc.gpsimd.dma_start(
@@ -88,8 +88,6 @@ def tile_list_tabglu_tm_none_kernel(tc, tab, w4_words, w4_scales, w8, offs, out)
         load_w4(w4_first, 0, PASSES, 0)
         load_table(2, 2 * TABLE_BYTES)
         load_table(3, 3 * TABLE_BYTES)
-        w4_late = keep.tile([P, PASSES, HALF // 2], I32, align_bytes=256, name="w4_late")
-        load_w4(w4_late, 0, PASSES, 1)
 
         picked = [keep.tile([P, S], U32, align_bytes=256, name=f"picked{a}") for a in range(PASSES)]
 
@@ -104,9 +102,12 @@ def tile_list_tabglu_tm_none_kernel(tc, tab, w4_words, w4_scales, w8, offs, out)
         picked_scales = keep.tile([P, S], U8, align_bytes=256, name="picked_scales")
         nc.vector.tensor_copy(picked_scales[:], table_scales[:].bitcast(U8).indirect(offsets[:]))
         for a in range(1, PASSES):
-            nc.scalar.dma_start(
+            engine = nc.sync if a == PASSES - 1 else nc.scalar
+            engine.dma_start(
                 moved[0:112, (a - 1) * S // 4 : a * S // 4], picked_scales[4 * a : 4 * a + 112, :].bitcast(I32)
             )
+        w4_late = shared.tile([P, PASSES, HALF // 2], I32, align_bytes=256, offset=4 * TABLE_BYTES, name="w4_late")
+        load_w4(w4_late, 0, PASSES, 1)
         moved_u8 = moved[:].bitcast(U8)
 
         def multiply(acc, a, t, rhs, rhs_scale):
@@ -139,7 +140,7 @@ def tile_list_tabglu_tm_none_kernel(tc, tab, w4_words, w4_scales, w8, offs, out)
 
         def load_w8(a, h):
             raw = shared.tile(
-                [P, 4, HALF], F32, align_bytes=256, offset=(PASSES * h + a) * RAW_BYTES, name=f"raw{a}{h}"
+                [P, 4, HALF], F32, align_bytes=256, offset=(2 + (PASSES * h + a) % 6) * RAW_BYTES, name=f"raw{a}{h}"
             )
             nc.sync.dma_start(
                 raw[:], w8[512 * a : 512 * (a + 1), h * HALF : (h + 1) * HALF].rearrange("(p j) n -> p j n", j=4)
@@ -173,11 +174,15 @@ def tile_list_tabglu_tm_none_kernel(tc, tab, w4_words, w4_scales, w8, offs, out)
             nc.vector.tensor_tensor(res[:], acc[:], gates[t, h][:, cols], MULT)
             nc.sync.dma_start(out[t * P : (t + 1) * P, h * HALF + cols.start : h * HALF + cols.stop], res[:])
 
-        accs = [psum.tile([P, HALF], F32, name="acc") for t in range(TOKENS)]
+        def bank(b, width=HALF):
+            return psum.tile([P, width], F32, name=f"bank{b}")
+
+        accs = [bank(t) for t in range(TOKENS)]
         for a in range(PASSES):
             gather_words(a, 2 if a == PASSES - 1 else 1)
-            load_w8(2 * a % PASSES, a // 2)
-            load_w8(2 * a % PASSES + 1, a // 2)
+            if a > 0:
+                load_w8(2 * (a - 1) % PASSES, (a - 1) // 2)
+                load_w8(2 * (a - 1) % PASSES + 1, (a - 1) // 2)
             for t in range(TOKENS):
                 mm_w4(accs[t], a, t, 0)
         for t in range(TOKENS):
@@ -186,7 +191,9 @@ def tile_list_tabglu_tm_none_kernel(tc, tab, w4_words, w4_scales, w8, offs, out)
         for t in range(TOKENS):
             if t % 2 == 1:
                 quantize_w8(t // 2, 0)
-            acc = psum.tile([P, HALF], F32, name="acc")
+                if t // 2 < 2:
+                    load_w8(2 + t // 2, 1)
+            acc = bank(t)
             for a in range(PASSES):
                 mm_w4(acc, a, t, 1)
             gate(acc, t, 1)
@@ -194,7 +201,7 @@ def tile_list_tabglu_tm_none_kernel(tc, tab, w4_words, w4_scales, w8, offs, out)
         for h in range(2):
             waiting = []
             for t in range(TOKENS - h):
-                acc = psum.tile([P, HALF], F32, name="acc")
+                acc = bank(t if h == 0 else t % AHEAD)
                 for a in range(PASSES - 1):
                     mm_w8(acc, a, t, h)
                 waiting.append((acc, t))
@@ -208,7 +215,7 @@ def tile_list_tabglu_tm_none_kernel(tc, tab, w4_words, w4_scales, w8, offs, out)
         t = TOKENS - 1
         n = HALF // 2
         for part in range(2):
-            acc = psum.tile([P, n], F32, name="acc")
+            acc = bank(part, n)
             cols = slice(part * n, (part + 1) * n)
             for a in range(PASSES):
                 mm_w8(acc, a, t, 1, cols)

@@ -37,6 +37,12 @@ def tile_list_tabglu_tm_none_kernel(tc, tab, w4_words, w4_scales, w8, offs, out)
         stage = ctx.enter_context(tc.tile_pool(name="stage", bufs=4))
         psum = ctx.enter_context(tc.psum_pool(name="psum", bufs=1))
 
+        table_scales = shared.tile([P, T // 4], I32, align_bytes=256, offset=46 * KIB, name="table_scales")
+        for a in range(PASSES):
+            nc.sync.dma_start(
+                table_scales[32 + a : 96 : 4, :],
+                tab[a, words_bytes : words_bytes + 16 * T].rearrange("(q t) -> q t", q=16).bitcast(I32),
+            )
         offsets = keep.tile([P, S // 16], U16, name="offsets")
         nc.sync.dma_start(offsets[:], offs)
 
@@ -50,23 +56,17 @@ def tile_list_tabglu_tm_none_kernel(tc, tab, w4_words, w4_scales, w8, offs, out)
 
         w4_codes = {}
 
-        def load_w4(tile, a0, a1, h):
-            nc.sync.dma_start(
+        def load_w4(engine, tile, a0, a1, h):
+            engine.dma_start(
                 tile[:], w4_words[a0:a1, :, h * 2 * HALF : (h + 1) * 2 * HALF].rearrange("a p x -> p a x").bitcast(I32)
             )
             for a in range(a0, a1):
                 w4_codes[a, h] = tile[:, a - a0, :]
 
         load_table(0, 0)
-        table_scales = shared.tile([P, T // 4], I32, align_bytes=256, offset=4 * TABLE_BYTES, name="table_scales")
-        nc.vector.memset(table_scales[:], 0)
-        for q in range(4):
-            nc.gpsimd.dma_start(
-                table_scales[32 * q : 32 * q + 16, :],
-                tab[:, words_bytes + 4 * q * T : words_bytes + (4 * q + 4) * T]
-                .rearrange("a (r t) -> a r t", r=4)
-                .bitcast(I32),
-            )
+        load_table(1, TABLE_BYTES)
+        w4_first = keep.tile([P, PASSES, HALF // 2], I32, align_bytes=256, name="w4_first")
+        load_w4(nc.gpsimd, w4_first, 0, PASSES, 0)
         planes = keep.tile([P, PASSES, M // 4], I32, align_bytes=256, name="planes")
         nc.vector.memset(planes[:], 0)
         for q in range(4):
@@ -75,19 +75,15 @@ def tile_list_tabglu_tm_none_kernel(tc, tab, w4_words, w4_scales, w8, offs, out)
                 w4_scales[:, 4 * q : 4 * q + 4, :].rearrange("a r n -> r a n").bitcast(I32),
             )
         planes_u8 = planes[:].rearrange("p a n -> p (a n)").bitcast(U8)
-        moved = keep.tile([P, (PASSES - 1) * S // 4], I32, align_bytes=256, name="moved")
+        nc.vector.memset(table_scales[0:32, :], 0)
+        nc.vector.memset(table_scales[96:P, :], 0)
+        moved = keep.tile([P, PASSES * S // 4], I32, align_bytes=256, name="moved")
         nc.vector.memset(moved[:], 0)
 
         warm = keep.tile([P, 1], F32, name="warm")
         nc.vector.memset(warm[:], 0.0)
         warm_out = keep.tile([P, 1], F32, name="warm_out")
         nc.scalar.activation(warm_out[:], warm[:], SILU)
-
-        load_table(1, TABLE_BYTES)
-        w4_first = keep.tile([P, PASSES, HALF // 2], I32, align_bytes=256, name="w4_first")
-        load_w4(w4_first, 0, PASSES, 0)
-        load_table(2, 2 * TABLE_BYTES)
-        load_table(3, 3 * TABLE_BYTES)
 
         picked = [keep.tile([P, S], U32, align_bytes=256, name=f"picked{a}") for a in range(PASSES)]
 
@@ -101,21 +97,18 @@ def tile_list_tabglu_tm_none_kernel(tc, tab, w4_words, w4_scales, w8, offs, out)
 
         picked_scales = keep.tile([P, S], U8, align_bytes=256, name="picked_scales")
         nc.vector.tensor_copy(picked_scales[:], table_scales[:].bitcast(U8).indirect(offsets[:]))
-        for a in range(1, PASSES):
-            engine = nc.sync if a == PASSES - 1 else nc.scalar
-            engine.dma_start(
-                moved[0:112, (a - 1) * S // 4 : a * S // 4], picked_scales[4 * a : 4 * a + 112, :].bitcast(I32)
+        for move in range(4 * PASSES):
+            if move in (6, 12):
+                load_table(1 + move // 6, (1 + move // 6) * TABLE_BYTES)
+            a, r = divmod(move, 4)
+            nc.sync.dma_start(
+                moved[r:P:32, a * S // 4 : (a + 1) * S // 4], picked_scales[32 + 4 * r + a : 96 : 16, :].bitcast(I32)
             )
-        w4_late = shared.tile([P, PASSES, HALF // 2], I32, align_bytes=256, offset=4 * TABLE_BYTES, name="w4_late")
-        load_w4(w4_late, 0, PASSES, 1)
         moved_u8 = moved[:].bitcast(U8)
 
         def multiply(acc, a, t, rhs, rhs_scale):
             cols = slice(t * P, (t + 1) * P)
-            if a == 0:
-                scales = picked_scales[:, cols]
-            else:
-                scales = moved_u8[:, (a - 1) * S + t * P : (a - 1) * S + (t + 1) * P]
+            scales = moved_u8[:, a * S + t * P : a * S + (t + 1) * P]
             nc.tensor.matmul_mx(
                 out=acc[:],
                 lhsT=picked[a][:, cols].bitcast(FP8X4),
@@ -140,7 +133,7 @@ def tile_list_tabglu_tm_none_kernel(tc, tab, w4_words, w4_scales, w8, offs, out)
 
         def load_w8(a, h):
             raw = shared.tile(
-                [P, 4, HALF], F32, align_bytes=256, offset=(2 + (PASSES * h + a) % 6) * RAW_BYTES, name=f"raw{a}{h}"
+                [P, 4, HALF], F32, align_bytes=256, offset=4 * KIB + (PASSES * h + a) * RAW_BYTES, name=f"raw{a}{h}"
             )
             nc.sync.dma_start(
                 raw[:], w8[512 * a : 512 * (a + 1), h * HALF : (h + 1) * HALF].rearrange("(p j) n -> p j n", j=4)
@@ -180,9 +173,11 @@ def tile_list_tabglu_tm_none_kernel(tc, tab, w4_words, w4_scales, w8, offs, out)
         accs = [bank(t) for t in range(TOKENS)]
         for a in range(PASSES):
             gather_words(a, 2 if a == PASSES - 1 else 1)
-            if a > 0:
-                load_w8(2 * (a - 1) % PASSES, (a - 1) // 2)
-                load_w8(2 * (a - 1) % PASSES + 1, (a - 1) // 2)
+            if a == 0:
+                w4_late = shared.tile([P, PASSES, HALF // 2], I32, align_bytes=256, offset=0, name="w4_late")
+                load_w4(nc.sync, w4_late, 0, PASSES, 1)
+            for piece in range(max(2 * a - 1, 0), 2 * a + 1 + a // 3):
+                load_w8(piece % PASSES, piece // PASSES)
             for t in range(TOKENS):
                 mm_w4(accs[t], a, t, 0)
         for t in range(TOKENS):
@@ -191,8 +186,6 @@ def tile_list_tabglu_tm_none_kernel(tc, tab, w4_words, w4_scales, w8, offs, out)
         for t in range(TOKENS):
             if t % 2 == 1:
                 quantize_w8(t // 2, 0)
-                if t // 2 < 2:
-                    load_w8(2 + t // 2, 1)
             acc = bank(t)
             for a in range(PASSES):
                 mm_w4(acc, a, t, 1)

@@ -64,17 +64,22 @@ def tile_list_tabglu_tm_none_kernel(tc, tab, w4_words, w4_scales, w8, offs, out)
                 w4_codes[a, h] = tile[:, a - a0, :]
 
         load_table(0, 0)
-        load_table(1, TABLE_BYTES)
+        planes = {}
+
+        def load_planes(tile, h):
+            nc.vector.memset(tile[:], 0)
+            for r in range(4):
+                nc.sync.dma_start(
+                    tile[r:P:32, :, :],
+                    w4_scales[:, r:16:4, h * HALF : (h + 1) * HALF].rearrange("a q n -> q a n").bitcast(I32),
+                )
+            planes[h] = tile[:].rearrange("p a n -> p (a n)").bitcast(U8)
+
+        planes_first = keep.tile([P, PASSES, HALF // 4], I32, align_bytes=256, name="planes_first")
+        load_planes(planes_first, 0)
         w4_first = keep.tile([P, PASSES, HALF // 2], I32, align_bytes=256, name="w4_first")
-        load_w4(nc.gpsimd, w4_first, 0, PASSES, 0)
-        planes = keep.tile([P, PASSES, M // 4], I32, align_bytes=256, name="planes")
-        nc.vector.memset(planes[:], 0)
-        for q in range(4):
-            nc.gpsimd.dma_start(
-                planes[32 * q : 32 * q + 4, :, :],
-                w4_scales[:, 4 * q : 4 * q + 4, :].rearrange("a r n -> r a n").bitcast(I32),
-            )
-        planes_u8 = planes[:].rearrange("p a n -> p (a n)").bitcast(U8)
+        load_w4(nc.sync, w4_first, 0, PASSES, 0)
+        load_table(1, TABLE_BYTES)
         nc.vector.memset(table_scales[0:32, :], 0)
         nc.vector.memset(table_scales[96:P, :], 0)
         moved = keep.tile([P, PASSES * S // 4], I32, align_bytes=256, name="moved")
@@ -120,8 +125,7 @@ def tile_list_tabglu_tm_none_kernel(tc, tab, w4_words, w4_scales, w8, offs, out)
             )
 
         def mm_w4(acc, a, t, h):
-            at = a * M + h * HALF
-            multiply(acc, a, t, w4_codes[a, h].bitcast(U8).bitcast(FP4X4), planes_u8[:, at : at + HALF])
+            multiply(acc, a, t, w4_codes[a, h].bitcast(U8).bitcast(FP4X4), planes[h][:, a * HALF : (a + 1) * HALF])
 
         w8_codes = {}
 
@@ -133,7 +137,7 @@ def tile_list_tabglu_tm_none_kernel(tc, tab, w4_words, w4_scales, w8, offs, out)
 
         def load_w8(a, h):
             raw = shared.tile(
-                [P, 4, HALF], F32, align_bytes=256, offset=4 * KIB + (PASSES * h + a) * RAW_BYTES, name=f"raw{a}{h}"
+                [P, 4, HALF], F32, align_bytes=256, offset=6 * KIB + (PASSES * h + a) * RAW_BYTES, name=f"raw{a}{h}"
             )
             nc.sync.dma_start(
                 raw[:], w8[512 * a : 512 * (a + 1), h * HALF : (h + 1) * HALF].rearrange("(p j) n -> p j n", j=4)
@@ -176,6 +180,10 @@ def tile_list_tabglu_tm_none_kernel(tc, tab, w4_words, w4_scales, w8, offs, out)
             if a == 0:
                 w4_late = shared.tile([P, PASSES, HALF // 2], I32, align_bytes=256, offset=0, name="w4_late")
                 load_w4(nc.sync, w4_late, 0, PASSES, 1)
+                planes_late = shared.tile(
+                    [P, PASSES, HALF // 4], I32, align_bytes=256, offset=4 * KIB, name="planes_late"
+                )
+                load_planes(planes_late, 1)
             for piece in range(max(2 * a - 1, 0), 2 * a + 1 + a // 3):
                 load_w8(piece % PASSES, piece // PASSES)
             for t in range(TOKENS):

@@ -23,8 +23,8 @@ TOKENS = S // P
 KIB = 1024
 TABLE_BYTES = 4 * T
 RAW_BYTES = 4 * 4 * HALF
-SCALAR_COLUMNS = 384
-AHEAD = 4
+SCALAR_COLUMNS = [384, 384, 512, 512]
+AHEAD = 5
 
 
 def tile_list_tabglu_tm_none_kernel(tc, tab, w4_words, w4_scales, w8, offs, out):
@@ -145,13 +145,14 @@ def tile_list_tabglu_tm_none_kernel(tc, tab, w4_words, w4_scales, w8, offs, out)
             raws[a, h] = raw
 
         def quantize_w8(a, h):
-            cut = SCALAR_COLUMNS if h == 1 else 0
+            cut = SCALAR_COLUMNS[a] if h == 1 else 0
             grouped = stage.tile([P, HALF, 4], BF16, align_bytes=256, name="grouped")
             dst = grouped[:].rearrange("p (c i) t -> p c t i", i=4)
             src = raws[a, h][:].rearrange("p t (c i) -> p c t i", i=4)
             if cut:
                 nc.scalar.copy(dst[:, : cut // 4], src[:, : cut // 4])
-            nc.vector.tensor_copy(dst[:, cut // 4 :], src[:, cut // 4 :])
+            if cut < HALF:
+                nc.vector.tensor_copy(dst[:, cut // 4 :], src[:, cut // 4 :])
             codes = keep.tile([P, HALF], U32, align_bytes=256, name=f"w8_codes{a}{h}")
             scales = keep.tile([P, HALF], U8, align_bytes=256, name=f"w8_scales{a}{h}")
             nc.vector.quantize_mx(
@@ -216,7 +217,7 @@ def tile_list_tabglu_tm_none_kernel(tc, tab, w4_words, w4_scales, w8, offs, out)
         t = TOKENS - 1
         n = HALF // 2
         for part in range(2):
-            acc = bank(part, n)
+            acc = bank(TOKENS - 1 - AHEAD + part, n)
             cols = slice(part * n, (part + 1) * n)
             for a in range(PASSES):
                 mm_w8(acc, a, t, 1, cols)

@@ -50,9 +50,7 @@ def tile_list_tabglu_tm_none_kernel(tc, tab, w4_words, w4_scales, w8, offs, out)
 
         def load_table(a, at):
             table[a] = shared.tile([P, T], I32, align_bytes=256, offset=at, name=f"table{a}")
-            nc.sync.dma_start(
-                table[a][:], tab[a, 0:words_bytes].rearrange("(p x) -> p x", p=P).bitcast(I32), max_dma_last_dim=4 * KIB
-            )
+            nc.sync.dma_start(table[a][:], tab[a, 0:words_bytes].rearrange("(p x) -> p x", p=P).bitcast(I32))
 
         w4_codes = {}
 

@@ -24,7 +24,7 @@ KIB = 1024
 TABLE_BYTES = 4 * T
 RAW_BYTES = 4 * 4 * HALF
 SCALAR_COLUMNS = [384, 384, 512, 512]
-AHEAD = 5
+AHEAD = 4
 
 
 def tile_list_tabglu_tm_none_kernel(tc, tab, w4_words, w4_scales, w8, offs, out):
@@ -75,8 +75,8 @@ def tile_list_tabglu_tm_none_kernel(tc, tab, w4_words, w4_scales, w8, offs, out)
 
         planes_first = keep.tile([P, PASSES, HALF // 4], I32, align_bytes=256, name="planes_first")
         load_planes(planes_first, 0)
-        w4_first = keep.tile([P, PASSES, HALF // 2], I32, align_bytes=256, name="w4_first")
-        load_w4(nc.sync, w4_first, 0, PASSES, 0)
+        w4_first = keep.tile([P, PASSES - 1, HALF // 2], I32, align_bytes=256, name="w4_first")
+        load_w4(nc.sync, w4_first, 0, PASSES - 1, 0)
         load_table(1, TABLE_BYTES)
         nc.vector.memset(table_scales[0:32, :], 0)
         nc.vector.memset(table_scales[96:P, :], 0)
@@ -135,7 +135,7 @@ def tile_list_tabglu_tm_none_kernel(tc, tab, w4_words, w4_scales, w8, offs, out)
 
         def load_w8(a, h):
             raw = shared.tile(
-                [P, 4, HALF], F32, align_bytes=256, offset=6 * KIB + (PASSES * h + a) * RAW_BYTES, name=f"raw{a}{h}"
+                [P, 4, HALF], F32, align_bytes=256, offset=7 * KIB + (PASSES * h + a) * RAW_BYTES, name=f"raw{a}{h}"
             )
             nc.sync.dma_start(
                 raw[:], w8[512 * a : 512 * (a + 1), h * HALF : (h + 1) * HALF].rearrange("(p j) n -> p j n", j=4)
@@ -177,10 +177,16 @@ def tile_list_tabglu_tm_none_kernel(tc, tab, w4_words, w4_scales, w8, offs, out)
         for a in range(PASSES):
             gather_words(a, 2 if a == PASSES - 1 else 1)
             if a == 0:
-                w4_late = shared.tile([P, PASSES, HALF // 2], I32, align_bytes=256, offset=0, name="w4_late")
-                load_w4(nc.sync, w4_late, 0, PASSES, 1)
+                w4_last = shared.tile([P, HALF], I32, align_bytes=256, offset=0, name="w4_last")
+                nc.sync.dma_start(w4_last[:], w4_words[PASSES - 1].bitcast(I32))
+                for h in range(2):
+                    w4_codes[PASSES - 1, h] = w4_last[:, h * HALF // 2 : (h + 1) * HALF // 2]
+                w4_late = shared.tile(
+                    [P, PASSES - 1, HALF // 2], I32, align_bytes=256, offset=2 * KIB, name="w4_late"
+                )
+                load_w4(nc.sync, w4_late, 0, PASSES - 1, 1)
                 planes_late = shared.tile(
-                    [P, PASSES, HALF // 4], I32, align_bytes=256, offset=4 * KIB, name="planes_late"
+                    [P, PASSES, HALF // 4], I32, align_bytes=256, offset=5 * KIB, name="planes_late"
                 )
                 load_planes(planes_late, 1)
             for piece in range(max(2 * a - 1, 0), 2 * a + 1 + a // 3):
@@ -213,10 +219,8 @@ def tile_list_tabglu_tm_none_kernel(tc, tab, w4_words, w4_scales, w8, offs, out)
                 if h == 0 and t % 2 == 1:
                     quantize_w8(t // 2, 1)
         t = TOKENS - 1
-        n = HALF // 2
-        for part in range(2):
-            acc = bank(TOKENS - 1 - AHEAD + part, n)
-            cols = slice(part * n, (part + 1) * n)
+        for part, cols in enumerate([slice(0, 256), slice(256, 384), slice(384, 512)]):
+            acc = bank(TOKENS - 1 - AHEAD + part, cols.stop - cols.start)
             for a in range(PASSES):
                 mm_w8(acc, a, t, 1, cols)
             finish(acc, t, 1, cols)

@@ -35,6 +35,7 @@ def tile_list_tabglu_tm_none_kernel(tc, tab, w4_words, w4_scales, w8, offs, out)
         keep = ctx.enter_context(tc.tile_pool(name="keep", bufs=1))
         shared = ctx.enter_context(tc.tile_pool(name="shared", bufs=1))
         stage = ctx.enter_context(tc.tile_pool(name="stage", bufs=4))
+        late = ctx.enter_context(tc.tile_pool(name="late", bufs=1))
         psum = ctx.enter_context(tc.psum_pool(name="psum", bufs=1))
 
         table_scales = shared.tile([P, T // 4], I32, align_bytes=256, offset=46 * KIB, name="table_scales")
@@ -144,7 +145,10 @@ def tile_list_tabglu_tm_none_kernel(tc, tab, w4_words, w4_scales, w8, offs, out)
 
         def quantize_w8(a, h):
             cut = SCALAR_COLUMNS[a] if h == 1 else 0
-            grouped = stage.tile([P, HALF, 4], BF16, align_bytes=256, name="grouped")
+            if h == 0:
+                grouped = stage.tile([P, HALF, 4], BF16, align_bytes=256, name="grouped")
+            else:
+                grouped = late.tile([P, HALF, 4], BF16, align_bytes=256, offset=4 * KIB * a, name=f"grouped{a}")
             dst = grouped[:].rearrange("p (c i) t -> p c t i", i=4)
             src = raws[a, h][:].rearrange("p t (c i) -> p c t i", i=4)
             if cut:
@@ -166,7 +170,10 @@ def tile_list_tabglu_tm_none_kernel(tc, tab, w4_words, w4_scales, w8, offs, out)
             gates[t, h] = g
 
         def finish(acc, t, h, cols=slice(0, HALF)):
-            res = keep.tile([P, cols.stop - cols.start], F32, name=f"res{t}{h}{cols.start}")
+            if h == 0 and t >= AHEAD:
+                res = late.tile([P, HALF], F32, align_bytes=256, offset=4 * KIB * (t - AHEAD), name=f"res{t}")
+            else:
+                res = keep.tile([P, cols.stop - cols.start], F32, name=f"res{t}{h}{cols.start}")
             nc.vector.tensor_tensor(res[:], acc[:], gates[t, h][:, cols], MULT)
             nc.sync.dma_start(out[t * P : (t + 1) * P, h * HALF + cols.start : h * HALF + cols.stop], res[:])
 
@@ -207,6 +214,8 @@ def tile_list_tabglu_tm_none_kernel(tc, tab, w4_words, w4_scales, w8, offs, out)
         for h in range(2):
             waiting = []
             for t in range(TOKENS - h):
+                if h == 0 and t >= AHEAD:
+                    quantize_w8(t - AHEAD, 1)
                 acc = bank(t if h == 0 else t % AHEAD)
                 for a in range(PASSES - 1):
                     mm_w8(acc, a, t, h)
@@ -216,11 +225,9 @@ def tile_list_tabglu_tm_none_kernel(tc, tab, w4_words, w4_scales, w8, offs, out)
                         acc, tw = waiting.pop(0)
                         mm_w8(acc, PASSES - 1, tw, h)
                         finish(acc, tw, h)
-                if h == 0 and t % 2 == 1:
-                    quantize_w8(t // 2, 1)
         t = TOKENS - 1
         for part, cols in enumerate([slice(0, 256), slice(256, 384), slice(384, 512)]):
-            acc = bank(TOKENS - 1 - AHEAD + part, cols.stop - cols.start)
+            acc = bank((TOKENS - 1 + part) % AHEAD, cols.stop - cols.start)
             for a in range(PASSES):
                 mm_w8(acc, a, t, 1, cols)
             finish(acc, t, 1, cols)

@@ -23,7 +23,7 @@ TOKENS = S // P
 KIB = 1024
 TABLE_BYTES = 4 * T
 RAW_BYTES = 4 * 4 * HALF
-SCALAR_COLUMNS = [384, 384, 512, 512]
+SCALAR_COLUMNS = [384, 384, 384, 256]
 AHEAD = 4
 
 

@@ -39,11 +39,9 @@ def tile_list_tabglu_tm_none_kernel(tc, tab, w4_words, w4_scales, w8, offs, out)
         psum = ctx.enter_context(tc.psum_pool(name="psum", bufs=1))
 
         table_scales = shared.tile([P, T // 4], I32, align_bytes=256, offset=46 * KIB, name="table_scales")
-        for a in range(PASSES):
-            nc.sync.dma_start(
-                table_scales[32 + a : 96 : 4, :],
-                tab[a, words_bytes : words_bytes + 16 * T].rearrange("(q t) -> q t", q=16).bitcast(I32),
-            )
+        nc.sync.dma_start(
+            table_scales[32:96, :], tab[:, words_bytes:].rearrange("a (q t) -> q a t", q=16).bitcast(I32)
+        )
         offsets = keep.tile([P, S // 16], U16, name="offsets")
         nc.sync.dma_start(offsets[:], offs)
 
@@ -169,13 +167,27 @@ def tile_list_tabglu_tm_none_kernel(tc, tab, w4_words, w4_scales, w8, offs, out)
             nc.scalar.activation(g[:], acc[:], SILU)
             gates[t, h] = g
 
+        joined = {}
+
         def finish(acc, t, h, cols=slice(0, HALF)):
-            if h == 0 and t >= AHEAD:
-                res = late.tile([P, HALF], F32, align_bytes=256, offset=4 * KIB * (t - AHEAD), name=f"res{t}")
-            else:
+            if h == 1:
                 res = keep.tile([P, cols.stop - cols.start], F32, name=f"res{t}{h}{cols.start}")
-            nc.vector.tensor_tensor(res[:], acc[:], gates[t, h][:, cols], MULT)
-            nc.sync.dma_start(out[t * P : (t + 1) * P, h * HALF + cols.start : h * HALF + cols.stop], res[:])
+                nc.vector.tensor_tensor(res[:], acc[:], gates[t, h][:, cols], MULT)
+                nc.sync.dma_start(out[t * P : (t + 1) * P, HALF + cols.start : HALF + cols.stop], res[:])
+                return
+            count = AHEAD if t < AHEAD else 1
+            first = t - t % count
+            if t == first:
+                if t < AHEAD:
+                    joined[first] = keep.tile([P, count, HALF], F32, name="res_first")
+                else:
+                    at = 4 * KIB * (t - AHEAD)
+                    joined[first] = late.tile([P, count, HALF], F32, align_bytes=256, offset=at, name=f"res{t}")
+            nc.vector.tensor_tensor(joined[first][:, t - first, :], acc[:], gates[t, h][:], MULT)
+            if t == first + count - 1:
+                nc.sync.dma_start(
+                    out[first * P : (t + 1) * P, 0:HALF].rearrange("(t p) n -> p t n", p=P), joined[first][:]
+                )
 
         def bank(b, width=HALF):
             return psum.tile([P, width], F32, name=f"bank{b}")

@@ -215,28 +215,25 @@ def tile_list_tabglu_tm_none_kernel(tc, tab, w4_words, w4_scales, w8, offs, out)
         for t in range(TOKENS):
             gate(accs[t], t, 0)
 
-        for t in range(TOKENS):
-            if t % 2 == 1:
-                quantize_w8(t // 2, 0)
-            acc = bank(t)
+        for first in range(0, TOKENS, 2):
+            quantize_w8(first // 2, 0)
+            pair = [(bank(t), t) for t in (first, first + 1)]
             for a in range(PASSES):
-                mm_w4(acc, a, t, 1)
-            gate(acc, t, 1)
+                for acc, t in pair:
+                    mm_w4(acc, a, t, 1)
+            for acc, t in pair:
+                gate(acc, t, 1)
 
         for h in range(2):
-            waiting = []
-            for t in range(TOKENS - h):
-                if h == 0 and t >= AHEAD:
-                    quantize_w8(t - AHEAD, 1)
-                acc = bank(t if h == 0 else t % AHEAD)
-                for a in range(PASSES - 1):
-                    mm_w8(acc, a, t, h)
-                waiting.append((acc, t))
-                if t >= AHEAD - 1:
-                    while waiting:
-                        acc, tw = waiting.pop(0)
-                        mm_w8(acc, PASSES - 1, tw, h)
-                        finish(acc, tw, h)
+            for group in [(0, 1, 2, 3), (4, 5), (6, 7)[: 2 - h]]:
+                accs = [(bank(t if h == 0 else t % AHEAD), t) for t in group]
+                for a in range(PASSES):
+                    for acc, t in accs:
+                        mm_w8(acc, a, t, h)
+                for acc, t in accs:
+                    if h == 0 and t >= AHEAD:
+                        quantize_w8(t - AHEAD, 1)
+                    finish(acc, t, h)
         t = TOKENS - 1
         for part, cols in enumerate([slice(0, 256), slice(256, 384), slice(384, 512)]):
             acc = bank((TOKENS - 1 + part) % AHEAD, cols.stop - cols.start)

@@ -18,225 +18,218 @@ MULT = mybir.AluOpType.mult
 
 P = 128
 PASSES = K // 512
-HALF = 512
-TOKENS = S // P
-KIB = 1024
+LAST = PASSES - 1
+HALF = M // 2
+TOKEN_TILES = S // P
+ALIGN = 256
+
 TABLE_BYTES = 4 * T
+SCALE_ROWS_AT = 3 * TABLE_BYTES - T // 2
+W4_LAST_AT = 0
+W4_LATE_AT = W4_LAST_AT + 2 * M
+PLANES_LATE_AT = W4_LATE_AT + LAST * 2 * HALF
+RAW_AT = PLANES_LATE_AT + PASSES * HALF
 RAW_BYTES = 4 * 4 * HALF
-SCALAR_COLUMNS = [384, 384, 384, 256]
+GROUPED_BYTES = 2 * 4 * HALF
+
+MOVES_BETWEEN = 6
 AHEAD = 4
+TILE_GROUPS = [(0, 1, 2, 3), (4, 5), (6, 7)]
+SCALAR_COLUMNS = [384, 384, 384, 256]
+LAST_PARTS = [slice(0, 256), slice(256, 384), slice(384, 512)]
 
 
 def tile_list_tabglu_tm_none_kernel(tc, tab, w4_words, w4_scales, w8, offs, out):
     nc = tc.nc
-    words_bytes = 512 * T
+    words_bytes = P * TABLE_BYTES
 
     with ExitStack() as ctx:
         keep = ctx.enter_context(tc.tile_pool(name="keep", bufs=1))
         shared = ctx.enter_context(tc.tile_pool(name="shared", bufs=1))
-        stage = ctx.enter_context(tc.tile_pool(name="stage", bufs=4))
+        stage = ctx.enter_context(tc.tile_pool(name="stage", bufs=PASSES))
         late = ctx.enter_context(tc.tile_pool(name="late", bufs=1))
         psum = ctx.enter_context(tc.psum_pool(name="psum", bufs=1))
 
-        table_scales = shared.tile([P, T // 4], I32, align_bytes=256, offset=46 * KIB, name="table_scales")
-        nc.sync.dma_start(
-            table_scales[32:96, :], tab[:, words_bytes:].rearrange("a (q t) -> q a t", q=16).bitcast(I32)
-        )
-        offsets = keep.tile([P, S // 16], U16, name="offsets")
-        nc.sync.dma_start(offsets[:], offs)
-
         table = {}
+        w4_codes = {}
+        w4_planes = {}
+        raws = {}
+        w8_codes = {}
+        gates = {}
 
-        def load_table(a, at):
-            table[a] = shared.tile([P, T], I32, align_bytes=256, offset=at, name=f"table{a}")
+        def load_table(a):
+            table[a] = shared.tile([P, T], I32, align_bytes=ALIGN, offset=a * TABLE_BYTES, name=f"table{a}")
             nc.sync.dma_start(table[a][:], tab[a, 0:words_bytes].rearrange("(p x) -> p x", p=P).bitcast(I32))
 
-        w4_codes = {}
+        def load_w4(tile, h):
+            words = w4_words[0:LAST, :, h * 2 * HALF : (h + 1) * 2 * HALF]
+            nc.sync.dma_start(tile[:], words.rearrange("a p x -> p a x").bitcast(I32))
+            for a in range(LAST):
+                w4_codes[a, h] = tile[:, a, :]
 
-        def load_w4(engine, tile, a0, a1, h):
-            engine.dma_start(
-                tile[:], w4_words[a0:a1, :, h * 2 * HALF : (h + 1) * 2 * HALF].rearrange("a p x -> p a x").bitcast(I32)
-            )
-            for a in range(a0, a1):
-                w4_codes[a, h] = tile[:, a - a0, :]
-
-        load_table(0, 0)
-        planes = {}
-
-        def load_planes(tile, h):
+        def load_w4_planes(tile, h):
             nc.vector.memset(tile[:], 0)
             for r in range(4):
                 nc.sync.dma_start(
                     tile[r:P:32, :, :],
                     w4_scales[:, r:16:4, h * HALF : (h + 1) * HALF].rearrange("a q n -> q a n").bitcast(I32),
                 )
-            planes[h] = tile[:].rearrange("p a n -> p (a n)").bitcast(U8)
+            w4_planes[h] = tile[:].rearrange("p a n -> p (a n)").bitcast(U8)
 
-        planes_first = keep.tile([P, PASSES, HALF // 4], I32, align_bytes=256, name="planes_first")
-        load_planes(planes_first, 0)
-        w4_first = keep.tile([P, PASSES - 1, HALF // 2], I32, align_bytes=256, name="w4_first")
-        load_w4(nc.sync, w4_first, 0, PASSES - 1, 0)
-        load_table(1, TABLE_BYTES)
-        nc.vector.memset(table_scales[0:32, :], 0)
-        nc.vector.memset(table_scales[96:P, :], 0)
-        moved = keep.tile([P, PASSES * S // 4], I32, align_bytes=256, name="moved")
-        nc.vector.memset(moved[:], 0)
+        scale_rows = shared.tile([P, T // 4], I32, align_bytes=ALIGN, offset=SCALE_ROWS_AT, name="scale_rows")
+        nc.sync.dma_start(scale_rows[32:96, :], tab[:, words_bytes:].rearrange("a (q t) -> q a t", q=16).bitcast(I32))
+        offsets = keep.tile([P, S // 16], U16, name="offsets")
+        nc.sync.dma_start(offsets[:], offs)
+        load_table(0)
+        planes_first = keep.tile([P, PASSES, HALF // 4], I32, align_bytes=ALIGN, name="planes_first")
+        load_w4_planes(planes_first, 0)
+        w4_first = keep.tile([P, LAST, HALF // 2], I32, align_bytes=ALIGN, name="w4_first")
+        load_w4(w4_first, 0)
+        load_table(1)
 
-        warm = keep.tile([P, 1], F32, name="warm")
-        nc.vector.memset(warm[:], 0.0)
-        warm_out = keep.tile([P, 1], F32, name="warm_out")
-        nc.scalar.activation(warm_out[:], warm[:], SILU)
-
-        picked = [keep.tile([P, S], U32, align_bytes=256, name=f"picked{a}") for a in range(PASSES)]
-
-        def gather_words(a, parts=1):
-            n = S // parts
-            for i in range(parts):
-                nc.vector.tensor_copy(
-                    picked[a][:, i * n : (i + 1) * n],
-                    table[a][:].bitcast(U32).indirect(offsets[:, i * n // 16 : (i + 1) * n // 16]),
-                )
-
-        picked_scales = keep.tile([P, S], U8, align_bytes=256, name="picked_scales")
-        nc.vector.tensor_copy(picked_scales[:], table_scales[:].bitcast(U8).indirect(offsets[:]))
+        nc.vector.memset(scale_rows[0:32, :], 0)
+        nc.vector.memset(scale_rows[96:P, :], 0)
+        table_planes = keep.tile([P, PASSES * S // 4], I32, align_bytes=ALIGN, name="table_planes")
+        nc.vector.memset(table_planes[:], 0)
+        picked_scales = keep.tile([P, S], U8, align_bytes=ALIGN, name="picked_scales")
+        nc.vector.tensor_copy(picked_scales[:], scale_rows[:].bitcast(U8).indirect(offsets[:]))
         for move in range(4 * PASSES):
-            if move in (6, 12):
-                load_table(1 + move // 6, (1 + move // 6) * TABLE_BYTES)
+            if move in (MOVES_BETWEEN, 2 * MOVES_BETWEEN):
+                load_table(1 + move // MOVES_BETWEEN)
             a, r = divmod(move, 4)
             nc.sync.dma_start(
-                moved[r:P:32, a * S // 4 : (a + 1) * S // 4], picked_scales[32 + 4 * r + a : 96 : 16, :].bitcast(I32)
+                table_planes[r:P:32, a * S // 4 : (a + 1) * S // 4],
+                picked_scales[32 + 4 * r + a : 96 : 16, :].bitcast(I32),
             )
-        moved_u8 = moved[:].bitcast(U8)
+        table_planes_u8 = table_planes[:].bitcast(U8)
 
-        def multiply(acc, a, t, rhs, rhs_scale):
-            cols = slice(t * P, (t + 1) * P)
-            scales = moved_u8[:, a * S + t * P : a * S + (t + 1) * P]
-            nc.tensor.matmul_mx(
-                out=acc[:],
-                lhsT=picked[a][:, cols].bitcast(FP8X4),
-                lhsT_scale=scales,
-                rhs=rhs,
-                rhs_scale=rhs_scale,
-                start=(a == 0),
-                stop=(a == PASSES - 1),
+        picked = [keep.tile([P, S], U32, align_bytes=ALIGN, name=f"picked{a}") for a in range(PASSES)]
+
+        def gather_words(a):
+            n = S // 2 if a == LAST else S
+            for first in range(0, S, n):
+                nc.vector.tensor_copy(
+                    picked[a][:, first : first + n],
+                    table[a][:].bitcast(U32).indirect(offsets[:, first // 16 : (first + n) // 16]),
+                )
+
+        def load_rest_of_w4():
+            w4_last = shared.tile([P, HALF], I32, align_bytes=ALIGN, offset=W4_LAST_AT, name="w4_last")
+            nc.sync.dma_start(w4_last[:], w4_words[LAST].bitcast(I32))
+            for h in range(2):
+                w4_codes[LAST, h] = w4_last[:, h * HALF // 2 : (h + 1) * HALF // 2]
+            w4_late = shared.tile([P, LAST, HALF // 2], I32, align_bytes=ALIGN, offset=W4_LATE_AT, name="w4_late")
+            load_w4(w4_late, 1)
+            planes_late = shared.tile(
+                [P, PASSES, HALF // 4], I32, align_bytes=ALIGN, offset=PLANES_LATE_AT, name="planes_late"
             )
+            load_w4_planes(planes_late, 1)
 
-        def mm_w4(acc, a, t, h):
-            multiply(acc, a, t, w4_codes[a, h].bitcast(U8).bitcast(FP4X4), planes[h][:, a * HALF : (a + 1) * HALF])
+        def load_w8(piece):
+            h, a = divmod(piece, PASSES)
+            at = RAW_AT + piece * RAW_BYTES
+            raws[a, h] = shared.tile([P, 4, HALF], F32, align_bytes=ALIGN, offset=at, name=f"raw{a}{h}")
+            rows = w8[512 * a : 512 * (a + 1), h * HALF : (h + 1) * HALF]
+            nc.sync.dma_start(raws[a, h][:], rows.rearrange("(p i) n -> p i n", i=4))
 
-        w8_codes = {}
-
-        def mm_w8(acc, a, t, h, cols=slice(0, HALF)):
-            codes, scales = w8_codes[a, h]
-            multiply(acc, a, t, codes[:, cols].bitcast(FP8X4), scales[:, cols])
-
-        raws = {}
-
-        def load_w8(a, h):
-            raw = shared.tile(
-                [P, 4, HALF], F32, align_bytes=256, offset=7 * KIB + (PASSES * h + a) * RAW_BYTES, name=f"raw{a}{h}"
-            )
-            nc.sync.dma_start(
-                raw[:], w8[512 * a : 512 * (a + 1), h * HALF : (h + 1) * HALF].rearrange("(p j) n -> p j n", j=4)
-            )
-            raws[a, h] = raw
+        def last_table_under(piece):
+            return min((RAW_AT + (piece + 1) * RAW_BYTES - 1) // TABLE_BYTES, LAST)
 
         def quantize_w8(a, h):
-            cut = SCALAR_COLUMNS[a] if h == 1 else 0
             if h == 0:
-                grouped = stage.tile([P, HALF, 4], BF16, align_bytes=256, name="grouped")
+                cut = 0
+                grouped = stage.tile([P, HALF, 4], BF16, align_bytes=ALIGN, name="grouped")
             else:
-                grouped = late.tile([P, HALF, 4], BF16, align_bytes=256, offset=4 * KIB * a, name=f"grouped{a}")
-            dst = grouped[:].rearrange("p (c i) t -> p c t i", i=4)
-            src = raws[a, h][:].rearrange("p t (c i) -> p c t i", i=4)
+                cut = SCALAR_COLUMNS[a] // 4
+                grouped = late.tile([P, HALF, 4], BF16, align_bytes=ALIGN, offset=a * GROUPED_BYTES, name=f"grouped{a}")
+            dst = grouped[:].rearrange("p (c d) i -> p c i d", d=4)
+            src = raws[a, h][:].rearrange("p i (c d) -> p c i d", d=4)
             if cut:
-                nc.scalar.copy(dst[:, : cut // 4], src[:, : cut // 4])
-            if cut < HALF:
-                nc.vector.tensor_copy(dst[:, cut // 4 :], src[:, cut // 4 :])
-            codes = keep.tile([P, HALF], U32, align_bytes=256, name=f"w8_codes{a}{h}")
-            scales = keep.tile([P, HALF], U8, align_bytes=256, name=f"w8_scales{a}{h}")
+                nc.scalar.copy(dst[:, :cut], src[:, :cut])
+            nc.vector.tensor_copy(dst[:, cut:], src[:, cut:])
+            codes = keep.tile([P, HALF], U32, align_bytes=ALIGN, name=f"w8_codes{a}{h}")
+            plane = keep.tile([P, HALF], U8, align_bytes=ALIGN, name=f"w8_plane{a}{h}")
             nc.vector.quantize_mx(
-                out=codes[:].bitcast(FP8X4), scales=scales[:], in_=grouped[:].rearrange("p n t -> p (n t)")
+                out=codes[:].bitcast(FP8X4), scales=plane[:], in_=grouped[:].rearrange("p n i -> p (n i)")
             )
-            w8_codes[a, h] = (codes, scales)
-
-        gates = {}
-
-        def gate(acc, t, h):
-            g = keep.tile([P, HALF], F32, align_bytes=256, name=f"gate{t}{h}")
-            nc.scalar.activation(g[:], acc[:], SILU)
-            gates[t, h] = g
-
-        joined = {}
-
-        def finish(acc, t, h, cols=slice(0, HALF)):
-            if h == 1:
-                res = keep.tile([P, cols.stop - cols.start], F32, name=f"res{t}{h}{cols.start}")
-                nc.vector.tensor_tensor(res[:], acc[:], gates[t, h][:, cols], MULT)
-                nc.sync.dma_start(out[t * P : (t + 1) * P, HALF + cols.start : HALF + cols.stop], res[:])
-                return
-            count = AHEAD if t < AHEAD else 1
-            first = t - t % count
-            if t == first:
-                if t < AHEAD:
-                    joined[first] = keep.tile([P, count, HALF], F32, name="res_first")
-                else:
-                    at = 4 * KIB * (t - AHEAD)
-                    joined[first] = late.tile([P, count, HALF], F32, align_bytes=256, offset=at, name=f"res{t}")
-            nc.vector.tensor_tensor(joined[first][:, t - first, :], acc[:], gates[t, h][:], MULT)
-            if t == first + count - 1:
-                nc.sync.dma_start(
-                    out[first * P : (t + 1) * P, 0:HALF].rearrange("(t p) n -> p t n", p=P), joined[first][:]
-                )
+            w8_codes[a, h] = (codes, plane)
 
         def bank(b, width=HALF):
             return psum.tile([P, width], F32, name=f"bank{b}")
 
-        accs = [bank(t) for t in range(TOKENS)]
+        def multiply(acc, a, t, rhs, rhs_scale):
+            nc.tensor.matmul_mx(
+                out=acc[:],
+                lhsT=picked[a][:, t * P : (t + 1) * P].bitcast(FP8X4),
+                lhsT_scale=table_planes_u8[:, a * S + t * P : a * S + (t + 1) * P],
+                rhs=rhs,
+                rhs_scale=rhs_scale,
+                start=(a == 0),
+                stop=(a == LAST),
+            )
+
+        def multiply_w4(acc, a, t, h):
+            multiply(acc, a, t, w4_codes[a, h].bitcast(U8).bitcast(FP4X4), w4_planes[h][:, a * HALF : (a + 1) * HALF])
+
+        def multiply_w8(acc, a, t, h, cols):
+            codes, plane = w8_codes[a, h]
+            multiply(acc, a, t, codes[:, cols].bitcast(FP8X4), plane[:, cols])
+
+        def gate(acc, t, h):
+            gates[t, h] = keep.tile([P, HALF], F32, align_bytes=ALIGN, name=f"gate{t}{h}")
+            nc.scalar.activation(gates[t, h][:], acc[:], SILU)
+
+        def finish(result, acc, t, h, cols):
+            nc.vector.tensor_tensor(result[:], acc[:], gates[t, h][:, cols], MULT)
+            nc.sync.dma_start(out[t * P : (t + 1) * P, h * HALF + cols.start : h * HALF + cols.stop], result[:])
+
+        accs = [bank(t) for t in range(TOKEN_TILES)]
         for a in range(PASSES):
-            gather_words(a, 2 if a == PASSES - 1 else 1)
+            gather_words(a)
             if a == 0:
-                w4_last = shared.tile([P, HALF], I32, align_bytes=256, offset=0, name="w4_last")
-                nc.sync.dma_start(w4_last[:], w4_words[PASSES - 1].bitcast(I32))
-                for h in range(2):
-                    w4_codes[PASSES - 1, h] = w4_last[:, h * HALF // 2 : (h + 1) * HALF // 2]
-                w4_late = shared.tile(
-                    [P, PASSES - 1, HALF // 2], I32, align_bytes=256, offset=2 * KIB, name="w4_late"
-                )
-                load_w4(nc.sync, w4_late, 0, PASSES - 1, 1)
-                planes_late = shared.tile(
-                    [P, PASSES, HALF // 4], I32, align_bytes=256, offset=5 * KIB, name="planes_late"
-                )
-                load_planes(planes_late, 1)
-            for piece in range(max(2 * a - 1, 0), 2 * a + 1 + a // 3):
-                load_w8(piece % PASSES, piece // PASSES)
-            for t in range(TOKENS):
-                mm_w4(accs[t], a, t, 0)
-        for t in range(TOKENS):
+                load_rest_of_w4()
+            for piece in range(2 * PASSES):
+                if last_table_under(piece) == a:
+                    load_w8(piece)
+            for t in range(TOKEN_TILES):
+                multiply_w4(accs[t], a, t, 0)
+        for t in range(TOKEN_TILES):
             gate(accs[t], t, 0)
 
-        for first in range(0, TOKENS, 2):
+        for first in range(0, TOKEN_TILES, 2):
             quantize_w8(first // 2, 0)
             pair = [(bank(t), t) for t in (first, first + 1)]
             for a in range(PASSES):
                 for acc, t in pair:
-                    mm_w4(acc, a, t, 1)
+                    multiply_w4(acc, a, t, 1)
             for acc, t in pair:
                 gate(acc, t, 1)
 
-        for h in range(2):
-            for group in [(0, 1, 2, 3), (4, 5), (6, 7)[: 2 - h]]:
-                accs = [(bank(t if h == 0 else t % AHEAD), t) for t in group]
-                for a in range(PASSES):
-                    for acc, t in accs:
-                        mm_w8(acc, a, t, h)
-                for acc, t in accs:
-                    if h == 0 and t >= AHEAD:
-                        quantize_w8(t - AHEAD, 1)
-                    finish(acc, t, h)
-        t = TOKENS - 1
-        for part, cols in enumerate([slice(0, 256), slice(256, 384), slice(384, 512)]):
-            acc = bank((TOKENS - 1 + part) % AHEAD, cols.stop - cols.start)
+        def multiply_group(group, h, banks):
+            accs = [(bank(t % banks), t) for t in group]
             for a in range(PASSES):
-                mm_w8(acc, a, t, 1, cols)
-            finish(acc, t, 1, cols)
+                for acc, t in accs:
+                    multiply_w8(acc, a, t, h, whole)
+            return accs
+
+        whole = slice(0, HALF)
+        results = keep.tile([P, AHEAD, HALF], F32, name="results")
+        for acc, t in multiply_group(TILE_GROUPS[0], 0, TOKEN_TILES):
+            nc.vector.tensor_tensor(results[:, t, :], acc[:], gates[t, 0][:], MULT)
+        nc.sync.dma_start(out[0 : AHEAD * P, 0:HALF].rearrange("(t p) n -> p t n", p=P), results[:])
+        for group in TILE_GROUPS[1:]:
+            for acc, t in multiply_group(group, 0, TOKEN_TILES):
+                quantize_w8(t - AHEAD, 1)
+                at = (t - AHEAD) * GROUPED_BYTES
+                finish(late.tile([P, HALF], F32, align_bytes=ALIGN, offset=at, name=f"late{t}"), acc, t, 0, whole)
+
+        last_tile = TOKEN_TILES - 1
+        for group in TILE_GROUPS:
+            for acc, t in multiply_group([t for t in group if t != last_tile], 1, AHEAD):
+                finish(keep.tile([P, HALF], F32, name=f"result{t}"), acc, t, 1, whole)
+        for part, cols in enumerate(LAST_PARTS):
+            width = cols.stop - cols.start
+            acc = bank((last_tile + part) % AHEAD, width)
+            for a in range(PASSES):
+                multiply_w8(acc, a, last_tile, 1, cols)
+            finish(keep.tile([P, width], F32, name=f"part{part}"), acc, last_tile, 1, cols)

@@ -91,6 +91,12 @@ def tile_list_tabglu_tm_none_kernel(tc, tab, w4_words, w4_scales, w8, offs, out)
         nc.vector.memset(scale_rows[96:P, :], 0)
         table_planes = keep.tile([P, PASSES * S // 4], I32, align_bytes=ALIGN, name="table_planes")
         nc.vector.memset(table_planes[:], 0)
+
+        warm = keep.tile([P, 1], F32, name="warm")
+        nc.vector.memset(warm[:], 0.0)
+        warm_out = keep.tile([P, 1], F32, name="warm_out")
+        nc.scalar.activation(warm_out[:], warm[:], SILU)
+
         picked_scales = keep.tile([P, S], U8, align_bytes=ALIGN, name="picked_scales")
         nc.vector.tensor_copy(picked_scales[:], scale_rows[:].bitcast(U8).indirect(offsets[:]))
         for move in range(4 * PASSES):

@@ -31,11 +31,12 @@ PLANES_LATE_AT = W4_LATE_AT + LAST * 2 * HALF
 RAW_AT = PLANES_LATE_AT + PASSES * HALF
 RAW_BYTES = 4 * 4 * HALF
 GROUPED_BYTES = 2 * 4 * HALF
+GROUPED_AT = [0, 2 * GROUPED_BYTES, 3 * GROUPED_BYTES, 4 * GROUPED_BYTES]
 
 MOVES_BETWEEN = 6
 AHEAD = 4
 TILE_GROUPS = [(0, 1, 2, 3), (4, 5), (6, 7)]
-SCALAR_COLUMNS = [384, 384, 384, 256]
+SCALAR_COLUMNS = [256, 384, 384, 256]
 LAST_PARTS = [slice(0, 256), slice(256, 384), slice(384, 512)]
 
 
@@ -147,7 +148,7 @@ def tile_list_tabglu_tm_none_kernel(tc, tab, w4_words, w4_scales, w8, offs, out)
                 grouped = stage.tile([P, HALF, 4], BF16, align_bytes=ALIGN, name="grouped")
             else:
                 cut = SCALAR_COLUMNS[a] // 4
-                grouped = late.tile([P, HALF, 4], BF16, align_bytes=ALIGN, offset=a * GROUPED_BYTES, name=f"grouped{a}")
+                grouped = late.tile([P, HALF, 4], BF16, align_bytes=ALIGN, offset=GROUPED_AT[a], name=f"grouped{a}")
             dst = grouped[:].rearrange("p (c d) i -> p c i d", d=4)
             src = raws[a, h][:].rearrange("p i (c d) -> p c i d", d=4)
             if cut:
@@ -219,14 +220,16 @@ def tile_list_tabglu_tm_none_kernel(tc, tab, w4_words, w4_scales, w8, offs, out)
             return accs
 
         whole = slice(0, HALF)
-        results = keep.tile([P, AHEAD, HALF], F32, name="results")
+        quantize_w8(0, 1)
+        results = late.tile([P, AHEAD, HALF], F32, align_bytes=ALIGN, offset=0, name="results")
         for acc, t in multiply_group(TILE_GROUPS[0], 0, TOKEN_TILES):
             nc.vector.tensor_tensor(results[:, t, :], acc[:], gates[t, 0][:], MULT)
         nc.sync.dma_start(out[0 : AHEAD * P, 0:HALF].rearrange("(t p) n -> p t n", p=P), results[:])
         for group in TILE_GROUPS[1:]:
             for acc, t in multiply_group(group, 0, TOKEN_TILES):
-                quantize_w8(t - AHEAD, 1)
-                at = (t - AHEAD) * GROUPED_BYTES
+                if t != 5:
+                    quantize_w8({4: 1, 6: 2, 7: 3}[t], 1)
+                at = {4: GROUPED_AT[1], 5: GROUPED_AT[1] + 4 * HALF, 6: GROUPED_AT[2], 7: GROUPED_AT[3]}[t]
                 finish(late.tile([P, HALF], F32, align_bytes=ALIGN, offset=at, name=f"late{t}"), acc, t, 0, whole)
 
         last_tile = TOKEN_TILES - 1

@@ -213,7 +213,7 @@ def tile_list_tabglu_tm_none_kernel(tc, tab, w4_words, w4_scales, w8, offs, out)
                 gate(acc, t, 1)
 
         def multiply_group(group, h, banks):
-            accs = [(bank(t % banks), t) for t in group]
+            accs = [(bank(banks[t % len(banks)]), t) for t in group]
             for a in range(PASSES):
                 for acc, t in accs:
                     multiply_w8(acc, a, t, h, whole)
@@ -222,23 +222,24 @@ def tile_list_tabglu_tm_none_kernel(tc, tab, w4_words, w4_scales, w8, offs, out)
         whole = slice(0, HALF)
         quantize_w8(0, 1)
         results = late.tile([P, AHEAD, HALF], F32, align_bytes=ALIGN, offset=0, name="results")
-        for acc, t in multiply_group(TILE_GROUPS[0], 0, TOKEN_TILES):
+        for acc, t in multiply_group(TILE_GROUPS[0], 0, range(TOKEN_TILES)):
             nc.vector.tensor_tensor(results[:, t, :], acc[:], gates[t, 0][:], MULT)
         nc.sync.dma_start(out[0 : AHEAD * P, 0:HALF].rearrange("(t p) n -> p t n", p=P), results[:])
         for group in TILE_GROUPS[1:]:
-            for acc, t in multiply_group(group, 0, TOKEN_TILES):
+            for acc, t in multiply_group(group, 0, range(TOKEN_TILES)):
                 if t != 5:
                     quantize_w8({4: 1, 6: 2, 7: 3}[t], 1)
                 at = {4: GROUPED_AT[1], 5: GROUPED_AT[1] + 4 * HALF, 6: GROUPED_AT[2], 7: GROUPED_AT[3]}[t]
                 finish(late.tile([P, HALF], F32, align_bytes=ALIGN, offset=at, name=f"late{t}"), acc, t, 0, whole)
 
         last_tile = TOKEN_TILES - 1
-        for group in TILE_GROUPS:
-            for acc, t in multiply_group([t for t in group if t != last_tile], 1, AHEAD):
+        ring = [0, 1, 2, last_tile]
+        for group in [(0, 1, 2), (3,), (4,), (5,), (6,)]:
+            for acc, t in multiply_group(group, 1, ring):
                 finish(keep.tile([P, HALF], F32, name=f"result{t}"), acc, t, 1, whole)
         for part, cols in enumerate(LAST_PARTS):
             width = cols.stop - cols.start
-            acc = bank((last_tile + part) % AHEAD, width)
+            acc = bank(ring[(last_tile + part) % len(ring)], width)
             for a in range(PASSES):
                 multiply_w8(acc, a, last_tile, 1, cols)
             finish(keep.tile([P, width], F32, name=f"part{part}"), acc, last_tile, 1, cols)

@@ -36,7 +36,7 @@ GROUPED_AT = [0, 2 * GROUPED_BYTES, 3 * GROUPED_BYTES, 4 * GROUPED_BYTES]
 MOVES_BETWEEN = 6
 AHEAD = 4
 TILE_GROUPS = [(0, 1, 2, 3), (4, 5), (6, 7)]
-SCALAR_COLUMNS = [256, 384, 384, 256]
+SCALAR_COLUMNS = [256, 384, 384, 192]
 LAST_PARTS = [slice(0, 256), slice(256, 384), slice(384, 512)]
 
 
@@ -233,8 +233,8 @@ def tile_list_tabglu_tm_none_kernel(tc, tab, w4_words, w4_scales, w8, offs, out)
                 finish(late.tile([P, HALF], F32, align_bytes=ALIGN, offset=at, name=f"late{t}"), acc, t, 0, whole)
 
         last_tile = TOKEN_TILES - 1
-        ring = [0, 1, 2, last_tile]
-        for group in [(0, 1, 2), (3,), (4,), (5,), (6,)]:
+        ring = [0, 1, 2, 3, last_tile]
+        for group in [(0, 1, 2, 3), (4,), (5,), (6,)]:
             for acc, t in multiply_group(group, 1, ring):
                 finish(keep.tile([P, HALF], F32, name=f"result{t}"), acc, t, 1, whole)
         for part, cols in enumerate(LAST_PARTS):

@@ -30,12 +30,15 @@ W4_LATE_AT = W4_LAST_AT + 2 * M
 PLANES_LATE_AT = W4_LATE_AT + LAST * 2 * HALF
 RAW_AT = PLANES_LATE_AT + PASSES * HALF
 RAW_BYTES = 4 * 4 * HALF
+
 GROUPED_BYTES = 2 * 4 * HALF
 GROUPED_AT = [0, 2 * GROUPED_BYTES, 3 * GROUPED_BYTES, 4 * GROUPED_BYTES]
 
 MOVES_BETWEEN = 6
 AHEAD = 4
-TILE_GROUPS = [(0, 1, 2, 3), (4, 5), (6, 7)]
+FIRST_HALF_GROUPS = [(0, 1, 2, 3), (4, 5), (6, 7)]
+PIECES_BEFORE = [(0,), (1,), (2, 3)]
+SECOND_HALF_BANKS = [0, 1, 2, 3, 6]
 SCALAR_COLUMNS = [256, 384, 384, 192]
 LAST_PARTS = [slice(0, 256), slice(256, 384), slice(384, 512)]
 
@@ -43,6 +46,7 @@ LAST_PARTS = [slice(0, 256), slice(256, 384), slice(384, 512)]
 def tile_list_tabglu_tm_none_kernel(tc, tab, w4_words, w4_scales, w8, offs, out):
     nc = tc.nc
     words_bytes = P * TABLE_BYTES
+    whole = slice(0, HALF)
 
     with ExitStack() as ctx:
         keep = ctx.enter_context(tc.tile_pool(name="keep", bufs=1))
@@ -186,9 +190,17 @@ def tile_list_tabglu_tm_none_kernel(tc, tab, w4_words, w4_scales, w8, offs, out)
             gates[t, h] = keep.tile([P, HALF], F32, align_bytes=ALIGN, name=f"gate{t}{h}")
             nc.scalar.activation(gates[t, h][:], acc[:], SILU)
 
-        def finish(result, acc, t, h, cols):
-            nc.vector.tensor_tensor(result[:], acc[:], gates[t, h][:, cols], MULT)
-            nc.sync.dma_start(out[t * P : (t + 1) * P, h * HALF + cols.start : h * HALF + cols.stop], result[:])
+        def multiply_group(group, h, banks):
+            sums = [(bank(banks[t % len(banks)]), t) for t in group]
+            for a in range(PASSES):
+                for acc, t in sums:
+                    multiply_w8(acc, a, t, h, whole)
+            return sums
+
+        def finish(acc, t, cols):
+            result = keep.tile([P, cols.stop - cols.start], F32, name=f"result{t}_{cols.start}")
+            nc.vector.tensor_tensor(result[:], acc[:], gates[t, 1][:, cols], MULT)
+            nc.sync.dma_start(out[t * P : (t + 1) * P, HALF + cols.start : HALF + cols.stop], result[:])
 
         accs = [bank(t) for t in range(TOKEN_TILES)]
         for a in range(PASSES):
@@ -212,34 +224,23 @@ def tile_list_tabglu_tm_none_kernel(tc, tab, w4_words, w4_scales, w8, offs, out)
             for acc, t in pair:
                 gate(acc, t, 1)
 
-        def multiply_group(group, h, banks):
-            accs = [(bank(banks[t % len(banks)]), t) for t in group]
-            for a in range(PASSES):
-                for acc, t in accs:
-                    multiply_w8(acc, a, t, h, whole)
-            return accs
-
-        whole = slice(0, HALF)
-        quantize_w8(0, 1)
-        results = late.tile([P, AHEAD, HALF], F32, align_bytes=ALIGN, offset=0, name="results")
-        for acc, t in multiply_group(TILE_GROUPS[0], 0, range(TOKEN_TILES)):
-            nc.vector.tensor_tensor(results[:, t, :], acc[:], gates[t, 0][:], MULT)
-        nc.sync.dma_start(out[0 : AHEAD * P, 0:HALF].rearrange("(t p) n -> p t n", p=P), results[:])
-        for group in TILE_GROUPS[1:]:
-            for acc, t in multiply_group(group, 0, range(TOKEN_TILES)):
-                if t != 5:
-                    quantize_w8({4: 1, 6: 2, 7: 3}[t], 1)
-                at = {4: GROUPED_AT[1], 5: GROUPED_AT[1] + 4 * HALF, 6: GROUPED_AT[2], 7: GROUPED_AT[3]}[t]
-                finish(late.tile([P, HALF], F32, align_bytes=ALIGN, offset=at, name=f"late{t}"), acc, t, 0, whole)
+        for group, pieces in zip(FIRST_HALF_GROUPS, PIECES_BEFORE):
+            sums = multiply_group(group, 0, range(TOKEN_TILES))
+            for a in pieces:
+                quantize_w8(a, 1)
+            at = GROUPED_AT[pieces[-1]]
+            results = late.tile([P, len(group), HALF], F32, align_bytes=ALIGN, offset=at, name=f"results{group[0]}")
+            for acc, t in sums:
+                nc.vector.tensor_tensor(results[:, t - group[0], :], acc[:], gates[t, 0][:], MULT)
+            rows = out[group[0] * P : (group[-1] + 1) * P, 0:HALF]
+            nc.sync.dma_start(rows.rearrange("(t p) n -> p t n", p=P), results[:])
 
         last_tile = TOKEN_TILES - 1
-        ring = [0, 1, 2, 3, last_tile]
-        for group in [(0, 1, 2, 3), (4,), (5,), (6,)]:
-            for acc, t in multiply_group(group, 1, ring):
-                finish(keep.tile([P, HALF], F32, name=f"result{t}"), acc, t, 1, whole)
+        for group in [range(AHEAD)] + [[t] for t in range(AHEAD, last_tile)]:
+            for acc, t in multiply_group(group, 1, SECOND_HALF_BANKS):
+                finish(acc, t, whole)
         for part, cols in enumerate(LAST_PARTS):
-            width = cols.stop - cols.start
-            acc = bank(ring[(last_tile + part) % len(ring)], width)
+            acc = bank(SECOND_HALF_BANKS[(last_tile + part) % len(SECOND_HALF_BANKS)], cols.stop - cols.start)
             for a in range(PASSES):
                 multiply_w8(acc, a, last_tile, 1, cols)
-            finish(keep.tile([P, width], F32, name=f"part{part}"), acc, last_tile, 1, cols)
+            finish(acc, last_tile, cols)

@@ -36,9 +36,8 @@ GROUPED_AT = [0, 2 * GROUPED_BYTES, 3 * GROUPED_BYTES, 4 * GROUPED_BYTES]
 
 MOVES_BETWEEN = 6
 AHEAD = 4
-FIRST_HALF_GROUPS = [(0, 1, 2, 3), (4, 5), (6, 7)]
-PIECES_BEFORE = [(0,), (1,), (2, 3)]
-SECOND_HALF_BANKS = [0, 1, 2, 3, 6]
+FIRST_HALF_GROUPS = [(0, 1, 2, 3), (4, 5), (6,), (7,)]
+SECOND_HALF_BANKS = [0, 1, 2, 3, 7]
 SCALAR_COLUMNS = [256, 384, 384, 192]
 LAST_PARTS = [slice(0, 256), slice(256, 384), slice(384, 512)]
 
@@ -224,12 +223,10 @@ def tile_list_tabglu_tm_none_kernel(tc, tab, w4_words, w4_scales, w8, offs, out)
             for acc, t in pair:
                 gate(acc, t, 1)
 
-        for group, pieces in zip(FIRST_HALF_GROUPS, PIECES_BEFORE):
+        for a, group in enumerate(FIRST_HALF_GROUPS):
             sums = multiply_group(group, 0, range(TOKEN_TILES))
-            for a in pieces:
-                quantize_w8(a, 1)
-            at = GROUPED_AT[pieces[-1]]
-            results = late.tile([P, len(group), HALF], F32, align_bytes=ALIGN, offset=at, name=f"results{group[0]}")
+            quantize_w8(a, 1)
+            results = late.tile([P, len(group), HALF], F32, align_bytes=ALIGN, offset=GROUPED_AT[a], name=f"results{a}")
             for acc, t in sums:
                 nc.vector.tensor_tensor(results[:, t - group[0], :], acc[:], gates[t, 0][:], MULT)
             rows = out[group[0] * P : (group[-1] + 1) * P, 0:HALF]

@@ -96,11 +96,6 @@ def tile_list_tabglu_tm_none_kernel(tc, tab, w4_words, w4_scales, w8, offs, out)
         table_planes = keep.tile([P, PASSES * S // 4], I32, align_bytes=ALIGN, name="table_planes")
         nc.vector.memset(table_planes[:], 0)
 
-        warm = keep.tile([P, 1], F32, name="warm")
-        nc.vector.memset(warm[:], 0.0)
-        warm_out = keep.tile([P, 1], F32, name="warm_out")
-        nc.scalar.activation(warm_out[:], warm[:], SILU)
-
         picked_scales = keep.tile([P, S], U8, align_bytes=ALIGN, name="picked_scales")
         nc.vector.tensor_copy(picked_scales[:], scale_rows[:].bitcast(U8).indirect(offsets[:]))
         for move in range(4 * PASSES):

@@ -38,7 +38,7 @@ MOVES_BETWEEN = 6
 AHEAD = 4
 FIRST_HALF_GROUPS = [(0, 1, 2, 3), (4, 5), (6,), (7,)]
 SECOND_HALF_BANKS = [0, 1, 2, 3, 7]
-SCALAR_COLUMNS = [256, 384, 384, 192]
+SCALAR_COLUMNS = [384, 448, 384, 192]
 LAST_PARTS = [slice(0, 256), slice(256, 384), slice(384, 512)]
 
 

@@ -98,14 +98,13 @@ def tile_list_tabglu_tm_none_kernel(tc, tab, w4_words, w4_scales, w8, offs, out)
 
         picked_scales = keep.tile([P, S], U8, align_bytes=ALIGN, name="picked_scales")
         nc.vector.tensor_copy(picked_scales[:], scale_rows[:].bitcast(U8).indirect(offsets[:]))
-        for move in range(4 * PASSES):
-            if move in (MOVES_BETWEEN, 2 * MOVES_BETWEEN):
-                load_table(1 + move // MOVES_BETWEEN)
-            a, r = divmod(move, 4)
+        for quadrant in range(4):
             nc.sync.dma_start(
-                table_planes[r:P:32, a * S // 4 : (a + 1) * S // 4],
-                picked_scales[32 + 4 * r + a : 96 : 16, :].bitcast(I32),
+                table_planes[32 * quadrant : 32 * quadrant + 4, :],
+                picked_scales[32 + 16 * quadrant : 48 + 16 * quadrant, :].bitcast(I32),
             )
+        load_table(2)
+        load_table(3)
         table_planes_u8 = table_planes[:].bitcast(U8)
 
         picked = [keep.tile([P, S], U32, align_bytes=ALIGN, name=f"picked{a}") for a in range(PASSES)]

@@ -227,11 +227,13 @@ def tile_list_tabglu_tm_none_kernel(tc, tab, w4_words, w4_scales, w8, offs, out)
             nc.sync.dma_start(rows.rearrange("(t p) n -> p t n", p=P), results[:])
 
         last_tile = TOKEN_TILES - 1
-        for group in [range(AHEAD)] + [[t] for t in range(AHEAD, last_tile)]:
+        for group in [range(AHEAD)] + [[t] for t in range(AHEAD, last_tile - 1)]:
             for acc, t in multiply_group(group, 1, SECOND_HALF_BANKS):
                 finish(acc, t, whole)
-        for part, cols in enumerate(LAST_PARTS):
-            acc = bank(SECOND_HALF_BANKS[(last_tile + part) % len(SECOND_HALF_BANKS)], cols.stop - cols.start)
+        parts = [(last_tile - 1, slice(0, 256)), (last_tile - 1, slice(256, 512))]
+        parts = parts + [(last_tile, cols) for cols in LAST_PARTS]
+        for part, (t, cols) in enumerate(parts):
+            acc = bank(SECOND_HALF_BANKS[(last_tile - 1 + part) % len(SECOND_HALF_BANKS)], cols.stop - cols.start)
             for a in range(PASSES):
-                multiply_w8(acc, a, last_tile, 1, cols)
-            finish(acc, last_tile, cols)
+                multiply_w8(acc, a, t, 1, cols)
+            finish(acc, t, cols)

@@ -98,7 +98,7 @@ def tile_list_tabglu_tm_none_kernel(tc, tab, w4_words, w4_scales, w8, offs, out)
 
         picked_scales = keep.tile([P, S], U8, align_bytes=ALIGN, name="picked_scales")
         nc.vector.tensor_copy(picked_scales[:], scale_rows[:].bitcast(U8).indirect(offsets[:]))
-        for quadrant in range(4):
+        for quadrant in (0, 2, 1, 3):
             nc.sync.dma_start(
                 table_planes[32 * quadrant : 32 * quadrant + 4, :],
                 picked_scales[32 + 16 * quadrant : 48 + 16 * quadrant, :].bitcast(I32),

@@ -26,8 +26,8 @@ ALIGN = 256
 TABLE_BYTES = 4 * T
 SCALE_ROWS_AT = 3 * TABLE_BYTES - T // 2
 W4_LAST_AT = 0
-W4_LATE_AT = W4_LAST_AT + 2 * M
-PLANES_LATE_AT = W4_LATE_AT + LAST * 2 * HALF
+W4_LATE_AT = W4_LAST_AT + 2 * HALF
+PLANES_LATE_AT = W4_LATE_AT + PASSES * 2 * HALF
 RAW_AT = PLANES_LATE_AT + PASSES * HALF
 RAW_BYTES = 4 * 4 * HALF
 
@@ -65,10 +65,10 @@ def tile_list_tabglu_tm_none_kernel(tc, tab, w4_words, w4_scales, w8, offs, out)
             table[a] = shared.tile([P, T], I32, align_bytes=ALIGN, offset=a * TABLE_BYTES, name=f"table{a}")
             nc.sync.dma_start(table[a][:], tab[a, 0:words_bytes].rearrange("(p x) -> p x", p=P).bitcast(I32))
 
-        def load_w4(tile, h):
-            words = w4_words[0:LAST, :, h * 2 * HALF : (h + 1) * 2 * HALF]
+        def load_w4(tile, h, passes):
+            words = w4_words[0:passes, :, h * 2 * HALF : (h + 1) * 2 * HALF]
             nc.sync.dma_start(tile[:], words.rearrange("a p x -> p a x").bitcast(I32))
-            for a in range(LAST):
+            for a in range(passes):
                 w4_codes[a, h] = tile[:, a, :]
 
         def load_w4_planes(tile, h):
@@ -88,7 +88,7 @@ def tile_list_tabglu_tm_none_kernel(tc, tab, w4_words, w4_scales, w8, offs, out)
         planes_first = keep.tile([P, PASSES, HALF // 4], I32, align_bytes=ALIGN, name="planes_first")
         load_w4_planes(planes_first, 0)
         w4_first = keep.tile([P, LAST, HALF // 2], I32, align_bytes=ALIGN, name="w4_first")
-        load_w4(w4_first, 0)
+        load_w4(w4_first, 0, LAST)
         load_table(1)
 
         nc.vector.memset(scale_rows[0:32, :], 0)
@@ -118,12 +118,11 @@ def tile_list_tabglu_tm_none_kernel(tc, tab, w4_words, w4_scales, w8, offs, out)
                 )
 
         def load_rest_of_w4():
-            w4_last = shared.tile([P, HALF], I32, align_bytes=ALIGN, offset=W4_LAST_AT, name="w4_last")
-            nc.sync.dma_start(w4_last[:], w4_words[LAST].bitcast(I32))
-            for h in range(2):
-                w4_codes[LAST, h] = w4_last[:, h * HALF // 2 : (h + 1) * HALF // 2]
-            w4_late = shared.tile([P, LAST, HALF // 2], I32, align_bytes=ALIGN, offset=W4_LATE_AT, name="w4_late")
-            load_w4(w4_late, 1)
+            w4_last = shared.tile([P, HALF // 2], I32, align_bytes=ALIGN, offset=W4_LAST_AT, name="w4_last")
+            nc.sync.dma_start(w4_last[:], w4_words[LAST, :, 0 : 2 * HALF].bitcast(I32))
+            w4_codes[LAST, 0] = w4_last[:]
+            w4_late = shared.tile([P, PASSES, HALF // 2], I32, align_bytes=ALIGN, offset=W4_LATE_AT, name="w4_late")
+            load_w4(w4_late, 1, PASSES)
             planes_late = shared.tile(
                 [P, PASSES, HALF // 4], I32, align_bytes=ALIGN, offset=PLANES_LATE_AT, name="planes_late"
             )

@@ -73,22 +73,22 @@ def tile_list_tabglu_tm_none_kernel(tc, tab, w4_words, w4_scales, w8, offs, out)
 
         def load_w4_planes(tile, h):
             nc.vector.memset(tile[:], 0)
-            for r in range(4):
-                nc.sync.dma_start(
-                    tile[r:P:32, :, :],
-                    w4_scales[:, r:16:4, h * HALF : (h + 1) * HALF].rearrange("a q n -> q a n").bitcast(I32),
-                )
+            blocks = [(r, 1) for r in range(4)] if h else [(0, 1), (1, 1), (2, 2), (6, 2), (3, 2), (7, 2)]
+            for q, step in blocks:
+                rows = w4_scales[:, q : 16 : 4 * step, h * HALF : (h + 1) * HALF]
+                first = 32 * (q // 4) + q % 4
+                nc.sync.dma_start(tile[first : P : 32 * step, :, :], rows.rearrange("a q n -> q a n").bitcast(I32))
             w4_planes[h] = tile[:].rearrange("p a n -> p (a n)").bitcast(U8)
 
         scale_rows = shared.tile([P, T // 4], I32, align_bytes=ALIGN, offset=SCALE_ROWS_AT, name="scale_rows")
         nc.sync.dma_start(scale_rows[32:96, :], tab[:, words_bytes:].rearrange("a (q t) -> q a t", q=16).bitcast(I32))
         offsets = keep.tile([P, S // 16], U16, name="offsets")
         nc.sync.dma_start(offsets[:], offs)
+        w4_first = keep.tile([P, LAST, HALF // 2], I32, align_bytes=ALIGN, name="w4_first")
+        load_w4(w4_first, 0, LAST)
         load_table(0)
         planes_first = keep.tile([P, PASSES, HALF // 4], I32, align_bytes=ALIGN, name="planes_first")
         load_w4_planes(planes_first, 0)
-        w4_first = keep.tile([P, LAST, HALF // 2], I32, align_bytes=ALIGN, name="w4_first")
-        load_w4(w4_first, 0, LAST)
         load_table(1)
 
         nc.vector.memset(scale_rows[0:32, :], 0)
@@ -98,7 +98,7 @@ def tile_list_tabglu_tm_none_kernel(tc, tab, w4_words, w4_scales, w8, offs, out)
 
         picked_scales = keep.tile([P, S], U8, align_bytes=ALIGN, name="picked_scales")
         nc.vector.tensor_copy(picked_scales[:], scale_rows[:].bitcast(U8).indirect(offsets[:]))
-        for quadrant in (0, 2, 1, 3):
+        for quadrant in (2, 0, 3, 1):
             nc.sync.dma_start(
                 table_planes[32 * quadrant : 32 * quadrant + 4, :],
                 picked_scales[32 + 16 * quadrant : 48 + 16 * quadrant, :].bitcast(I32),

@@ -34,12 +34,13 @@ RAW_BYTES = 4 * 4 * HALF
 GROUPED_BYTES = 2 * 4 * HALF
 GROUPED_AT = [0, 2 * GROUPED_BYTES, 3 * GROUPED_BYTES, 4 * GROUPED_BYTES]
 
-MOVES_BETWEEN = 6
+PAIRED_ROWS = 2
+W8_PLANE_FROM = 4
 AHEAD = 4
 FIRST_HALF_GROUPS = [(0, 1, 2, 3), (4, 5), (6,), (7,)]
 SECOND_HALF_BANKS = [0, 1, 2, 3, 7]
 SCALAR_COLUMNS = [384, 448, 384, 192]
-LAST_PARTS = [slice(0, 256), slice(256, 384), slice(384, 512)]
+LAST_PARTS = [(6, 0, 256), (6, 256, 512), (7, 0, 256), (7, 256, 384), (7, 384, 512)]
 
 
 def tile_list_tabglu_tm_none_kernel(tc, tab, w4_words, w4_scales, w8, offs, out):
@@ -71,13 +72,15 @@ def tile_list_tabglu_tm_none_kernel(tc, tab, w4_words, w4_scales, w8, offs, out)
             for a in range(passes):
                 w4_codes[a, h] = tile[:, a, :]
 
-        def load_w4_planes(tile, h):
+        def load_w4_planes(tile, h, paired_rows):
             nc.vector.memset(tile[:], 0)
-            blocks = [(r, 1) for r in range(4)] if h else [(0, 1), (1, 1), (2, 2), (6, 2), (3, 2), (7, 2)]
-            for q, step in blocks:
-                rows = w4_scales[:, q : 16 : 4 * step, h * HALF : (h + 1) * HALF]
-                first = 32 * (q // 4) + q % 4
-                nc.sync.dma_start(tile[first : P : 32 * step, :, :], rows.rearrange("a q n -> q a n").bitcast(I32))
+            for r in range(4):
+                step = 2 if r >= 4 - paired_rows else 1
+                for quadrant in range(step):
+                    rows = w4_scales[:, 4 * quadrant + r : 16 : 4 * step, h * HALF : (h + 1) * HALF]
+                    nc.sync.dma_start(
+                        tile[32 * quadrant + r : P : 32 * step, :, :], rows.rearrange("a q n -> q a n").bitcast(I32)
+                    )
             w4_planes[h] = tile[:].rearrange("p a n -> p (a n)").bitcast(U8)
 
         scale_rows = shared.tile([P, T // 4], I32, align_bytes=ALIGN, offset=SCALE_ROWS_AT, name="scale_rows")
@@ -88,7 +91,7 @@ def tile_list_tabglu_tm_none_kernel(tc, tab, w4_words, w4_scales, w8, offs, out)
         load_w4(w4_first, 0, LAST)
         load_table(0)
         planes_first = keep.tile([P, PASSES, HALF // 4], I32, align_bytes=ALIGN, name="planes_first")
-        load_w4_planes(planes_first, 0)
+        load_w4_planes(planes_first, 0, PAIRED_ROWS)
         load_table(1)
 
         nc.vector.memset(scale_rows[0:32, :], 0)
@@ -98,11 +101,12 @@ def tile_list_tabglu_tm_none_kernel(tc, tab, w4_words, w4_scales, w8, offs, out)
 
         picked_scales = keep.tile([P, S], U8, align_bytes=ALIGN, name="picked_scales")
         nc.vector.tensor_copy(picked_scales[:], scale_rows[:].bitcast(U8).indirect(offsets[:]))
-        for quadrant in (2, 0, 3, 1):
-            nc.sync.dma_start(
-                table_planes[32 * quadrant : 32 * quadrant + 4, :],
-                picked_scales[32 + 16 * quadrant : 48 + 16 * quadrant, :].bitcast(I32),
-            )
+        for low in range(2):
+            for quadrant in (low + 2, low):
+                nc.sync.dma_start(
+                    table_planes[32 * quadrant : 32 * quadrant + 4, :],
+                    picked_scales[32 + 16 * quadrant : 48 + 16 * quadrant, :].bitcast(I32),
+                )
         load_table(2)
         load_table(3)
         table_planes_u8 = table_planes[:].bitcast(U8)
@@ -126,7 +130,7 @@ def tile_list_tabglu_tm_none_kernel(tc, tab, w4_words, w4_scales, w8, offs, out)
             planes_late = shared.tile(
                 [P, PASSES, HALF // 4], I32, align_bytes=ALIGN, offset=PLANES_LATE_AT, name="planes_late"
             )
-            load_w4_planes(planes_late, 1)
+            load_w4_planes(planes_late, 1, 0)
 
         def load_w8(piece):
             h, a = divmod(piece, PASSES)
@@ -153,7 +157,9 @@ def tile_list_tabglu_tm_none_kernel(tc, tab, w4_words, w4_scales, w8, offs, out)
             codes = keep.tile([P, HALF], U32, align_bytes=ALIGN, name=f"w8_codes{a}{h}")
             plane = keep.tile([P, HALF], U8, align_bytes=ALIGN, name=f"w8_plane{a}{h}")
             nc.vector.quantize_mx(
-                out=codes[:].bitcast(FP8X4), scales=plane[:], in_=grouped[:].rearrange("p n i -> p (n i)")
+                out=codes[:].bitcast(FP8X4),
+                scales=plane[W8_PLANE_FROM:, :],
+                in_=grouped[:].rearrange("p n i -> p (n i)"),
             )
             w8_codes[a, h] = (codes, plane)
 
@@ -176,7 +182,7 @@ def tile_list_tabglu_tm_none_kernel(tc, tab, w4_words, w4_scales, w8, offs, out)
 
         def multiply_w8(acc, a, t, h, cols):
             codes, plane = w8_codes[a, h]
-            multiply(acc, a, t, codes[:, cols].bitcast(FP8X4), plane[:, cols])
+            multiply(acc, a, t, codes[:, cols].bitcast(FP8X4), plane[W8_PLANE_FROM:, cols])
 
         def gate(acc, t, h):
             gates[t, h] = keep.tile([P, HALF], F32, align_bytes=ALIGN, name=f"gate{t}{h}")
@@ -225,14 +231,12 @@ def tile_list_tabglu_tm_none_kernel(tc, tab, w4_words, w4_scales, w8, offs, out)
             rows = out[group[0] * P : (group[-1] + 1) * P, 0:HALF]
             nc.sync.dma_start(rows.rearrange("(t p) n -> p t n", p=P), results[:])
 
-        last_tile = TOKEN_TILES - 1
-        for group in [range(AHEAD)] + [[t] for t in range(AHEAD, last_tile - 1)]:
+        first_parted = LAST_PARTS[0][0]
+        for group in [range(AHEAD)] + [[t] for t in range(AHEAD, first_parted)]:
             for acc, t in multiply_group(group, 1, SECOND_HALF_BANKS):
                 finish(acc, t, whole)
-        parts = [(last_tile - 1, slice(0, 256)), (last_tile - 1, slice(256, 512))]
-        parts = parts + [(last_tile, cols) for cols in LAST_PARTS]
-        for part, (t, cols) in enumerate(parts):
-            acc = bank(SECOND_HALF_BANKS[(last_tile - 1 + part) % len(SECOND_HALF_BANKS)], cols.stop - cols.start)
+        for part, (t, start, stop) in enumerate(LAST_PARTS):
+            acc = bank(SECOND_HALF_BANKS[(first_parted + part) % len(SECOND_HALF_BANKS)], stop - start)
             for a in range(PASSES):
-                multiply_w8(acc, a, t, 1, cols)
-            finish(acc, t, cols)
+                multiply_w8(acc, a, t, 1, slice(start, stop))
+            finish(acc, t, slice(start, stop))

@@ -83,12 +83,12 @@ def tile_list_tabglu_tm_none_kernel(tc, tab, w4_words, w4_scales, w8, offs, out)
                     )
             w4_planes[h] = tile[:].rearrange("p a n -> p (a n)").bitcast(U8)
 
+        w4_first = keep.tile([P, LAST, HALF // 2], I32, align_bytes=ALIGN, name="w4_first")
+        load_w4(w4_first, 0, LAST)
         scale_rows = shared.tile([P, T // 4], I32, align_bytes=ALIGN, offset=SCALE_ROWS_AT, name="scale_rows")
         nc.sync.dma_start(scale_rows[32:96, :], tab[:, words_bytes:].rearrange("a (q t) -> q a t", q=16).bitcast(I32))
         offsets = keep.tile([P, S // 16], U16, name="offsets")
         nc.sync.dma_start(offsets[:], offs)
-        w4_first = keep.tile([P, LAST, HALF // 2], I32, align_bytes=ALIGN, name="w4_first")
-        load_w4(w4_first, 0, LAST)
         load_table(0)
         planes_first = keep.tile([P, PASSES, HALF // 4], I32, align_bytes=ALIGN, name="planes_first")
         load_w4_planes(planes_first, 0, PAIRED_ROWS)

@@ -213,14 +213,13 @@ def tile_list_tabglu_tm_none_kernel(tc, tab, w4_words, w4_scales, w8, offs, out)
         for t in range(TOKEN_TILES):
             gate(accs[t], t, 0)
 
-        for first in range(0, TOKEN_TILES, 2):
-            quantize_w8(first // 2, 0)
-            pair = [(bank(t), t) for t in (first, first + 1)]
+        for t in range(TOKEN_TILES):
+            if t % 2 == 0:
+                quantize_w8(t // 2, 0)
+            acc = bank(t)
             for a in range(PASSES):
-                for acc, t in pair:
-                    multiply_w4(acc, a, t, 1)
-            for acc, t in pair:
-                gate(acc, t, 1)
+                multiply_w4(acc, a, t, 1)
+            gate(acc, t, 1)
 
         for a, group in enumerate(FIRST_HALF_GROUPS):
             sums = multiply_group(group, 0, range(TOKEN_TILES))

@@ -39,7 +39,7 @@ W8_PLANE_FROM = 4
 AHEAD = 4
 FIRST_HALF_GROUPS = [(0, 1, 2, 3), (4, 5), (6,), (7,)]
 SECOND_HALF_BANKS = [0, 1, 2, 3, 7]
-SCALAR_COLUMNS = [384, 448, 384, 192]
+SCALAR_COLUMNS = HALF // 2
 LAST_PARTS = [(6, 0, 256), (6, 256, 512), (7, 0, 256), (7, 256, 384), (7, 384, 512)]
 
 
@@ -147,7 +147,7 @@ def tile_list_tabglu_tm_none_kernel(tc, tab, w4_words, w4_scales, w8, offs, out)
                 cut = 0
                 grouped = stage.tile([P, HALF, 4], BF16, align_bytes=ALIGN, name="grouped")
             else:
-                cut = SCALAR_COLUMNS[a] // 4
+                cut = SCALAR_COLUMNS // 4
                 grouped = late.tile([P, HALF, 4], BF16, align_bytes=ALIGN, offset=GROUPED_AT[a], name=f"grouped{a}")
             dst = grouped[:].rearrange("p (c d) i -> p c i d", d=4)
             src = raws[a, h][:].rearrange("p i (c d) -> p c i d", d=4)

@@ -35,7 +35,7 @@ GROUPED_BYTES = 2 * 4 * HALF
 GROUPED_AT = [0, 2 * GROUPED_BYTES, 3 * GROUPED_BYTES, 4 * GROUPED_BYTES]
 
 PAIRED_ROWS = 2
-W8_PLANE_FROM = 4
+W8_PLANE_FROM = 0
 AHEAD = 4
 FIRST_HALF_GROUPS = [(0, 1, 2, 3), (4, 5), (6,), (7,)]
 SECOND_HALF_BANKS = [0, 1, 2, 3, 7]

@@ -21,6 +21,8 @@ PASSES = K // 512
 LAST = PASSES - 1
 HALF = M // 2
 TOKEN_TILES = S // P
+QUADRANTS = 4
+BLOCKS = 4
 ALIGN = 256
 
 TABLE_BYTES = 4 * T
@@ -35,7 +37,6 @@ GROUPED_BYTES = 2 * 4 * HALF
 GROUPED_AT = [0, 2 * GROUPED_BYTES, 3 * GROUPED_BYTES, 4 * GROUPED_BYTES]
 
 PAIRED_ROWS = 2
-W8_PLANE_FROM = 0
 AHEAD = 4
 FIRST_HALF_GROUPS = [(0, 1, 2, 3), (4, 5), (6,), (7,)]
 SECOND_HALF_BANKS = [0, 1, 2, 3, 7]
@@ -74,10 +75,10 @@ def tile_list_tabglu_tm_none_kernel(tc, tab, w4_words, w4_scales, w8, offs, out)
 
         def load_w4_planes(tile, h, paired_rows):
             nc.vector.memset(tile[:], 0)
-            for r in range(4):
-                step = 2 if r >= 4 - paired_rows else 1
+            for r in range(BLOCKS):
+                step = 2 if r >= BLOCKS - paired_rows else 1
                 for quadrant in range(step):
-                    rows = w4_scales[:, 4 * quadrant + r : 16 : 4 * step, h * HALF : (h + 1) * HALF]
+                    rows = w4_scales[:, BLOCKS * quadrant + r : 16 : BLOCKS * step, h * HALF : (h + 1) * HALF]
                     nc.sync.dma_start(
                         tile[32 * quadrant + r : P : 32 * step, :, :], rows.rearrange("a q n -> q a n").bitcast(I32)
                     )
@@ -101,10 +102,10 @@ def tile_list_tabglu_tm_none_kernel(tc, tab, w4_words, w4_scales, w8, offs, out)
 
         picked_scales = keep.tile([P, S], U8, align_bytes=ALIGN, name="picked_scales")
         nc.vector.tensor_copy(picked_scales[:], scale_rows[:].bitcast(U8).indirect(offsets[:]))
-        for low in range(2):
+        for low in range(QUADRANTS // 2):
             for quadrant in (low + 2, low):
                 nc.sync.dma_start(
-                    table_planes[32 * quadrant : 32 * quadrant + 4, :],
+                    table_planes[32 * quadrant : 32 * quadrant + BLOCKS, :],
                     picked_scales[32 + 16 * quadrant : 48 + 16 * quadrant, :].bitcast(I32),
                 )
         load_table(2)
@@ -157,9 +158,7 @@ def tile_list_tabglu_tm_none_kernel(tc, tab, w4_words, w4_scales, w8, offs, out)
             codes = keep.tile([P, HALF], U32, align_bytes=ALIGN, name=f"w8_codes{a}{h}")
             plane = keep.tile([P, HALF], U8, align_bytes=ALIGN, name=f"w8_plane{a}{h}")
             nc.vector.quantize_mx(
-                out=codes[:].bitcast(FP8X4),
-                scales=plane[W8_PLANE_FROM:, :],
-                in_=grouped[:].rearrange("p n i -> p (n i)"),
+                out=codes[:].bitcast(FP8X4), scales=plane[:], in_=grouped[:].rearrange("p n i -> p (n i)")
             )
             w8_codes[a, h] = (codes, plane)
 
@@ -182,7 +181,7 @@ def tile_list_tabglu_tm_none_kernel(tc, tab, w4_words, w4_scales, w8, offs, out)
 
         def multiply_w8(acc, a, t, h, cols):
             codes, plane = w8_codes[a, h]
-            multiply(acc, a, t, codes[:, cols].bitcast(FP8X4), plane[W8_PLANE_FROM:, cols])
+            multiply(acc, a, t, codes[:, cols].bitcast(FP8X4), plane[:, cols])
 
         def gate(acc, t, h):
             gates[t, h] = keep.tile([P, HALF], F32, align_bytes=ALIGN, name=f"gate{t}{h}")

@@ -197,7 +197,8 @@ def tile_list_tabglu_tm_none_kernel(tc, tab, w4_words, w4_scales, w8, offs, out)
         def finish(acc, t, cols):
             result = keep.tile([P, cols.stop - cols.start], F32, name=f"result{t}_{cols.start}")
             nc.vector.tensor_tensor(result[:], acc[:], gates[t, 1][:, cols], MULT)
-            nc.sync.dma_start(out[t * P : (t + 1) * P, HALF + cols.start : HALF + cols.stop], result[:])
+            queue = nc.sync if t == TOKEN_TILES - 1 else nc.scalar
+            queue.dma_start(out[t * P : (t + 1) * P, HALF + cols.start : HALF + cols.stop], result[:])
 
         accs = [bank(t) for t in range(TOKEN_TILES)]
         for a in range(PASSES):

@@ -217,8 +217,9 @@ def tile_list_tabglu_tm_none_kernel(tc, tab, w4_words, w4_scales, w8, offs, out)
             if t % 2 == 0:
                 quantize_w8(t // 2, 0)
             acc = bank(t)
-            for a in range(PASSES):
-                multiply_w4(acc, a, t, 1)
+            for turn in range(4 if t == 2 else 1):
+                for a in range(PASSES):
+                    multiply_w4(acc, a, t, 1)
             gate(acc, t, 1)
 
         for a, group in enumerate(FIRST_HALF_GROUPS):

@@ -20,11 +20,8 @@ P = 128
 PASSES = K // 512
 LAST = PASSES - 1
 HALF = M // 2
-TOKEN_TILES = S // P
-QUADRANTS = 4
-BLOCKS = 4
+TILES = S // P
 ALIGN = 256
-
 TABLE_BYTES = 4 * T
 SCALE_ROWS_AT = 3 * TABLE_BYTES - T // 2
 W4_LAST_AT = 0
@@ -32,106 +29,84 @@ W4_LATE_AT = W4_LAST_AT + 2 * HALF
 PLANES_LATE_AT = W4_LATE_AT + PASSES * 2 * HALF
 RAW_AT = PLANES_LATE_AT + PASSES * HALF
 RAW_BYTES = 4 * 4 * HALF
-
-GROUPED_BYTES = 2 * 4 * HALF
-GROUPED_AT = [0, 2 * GROUPED_BYTES, 3 * GROUPED_BYTES, 4 * GROUPED_BYTES]
-
 PAIRED_ROWS = 2
 AHEAD = 4
-FIRST_HALF_GROUPS = [(0, 1, 2, 3), (4, 5), (6,), (7,)]
-SECOND_HALF_BANKS = [0, 1, 2, 3, 7]
-SCALAR_COLUMNS = HALF // 2
+SCALAR_COLUMNS = 7 * HALF // 8
+SECOND_BANKS = [0, 1, 2, 3, 6, 7]
 LAST_PARTS = [(6, 0, 256), (6, 256, 512), (7, 0, 256), (7, 256, 384), (7, 384, 512)]
 
 
 def tile_list_tabglu_tm_none_kernel(tc, tab, w4_words, w4_scales, w8, offs, out):
     nc = tc.nc
     words_bytes = P * TABLE_BYTES
-    whole = slice(0, HALF)
 
     with ExitStack() as ctx:
         keep = ctx.enter_context(tc.tile_pool(name="keep", bufs=1))
         shared = ctx.enter_context(tc.tile_pool(name="shared", bufs=1))
-        stage = ctx.enter_context(tc.tile_pool(name="stage", bufs=PASSES))
         late = ctx.enter_context(tc.tile_pool(name="late", bufs=1))
         psum = ctx.enter_context(tc.psum_pool(name="psum", bufs=1))
 
-        table = {}
-        w4_codes = {}
-        w4_planes = {}
+        table = [
+            shared.tile([P, T], I32, align_bytes=ALIGN, offset=a * TABLE_BYTES, name=f"table{a}") for a in range(PASSES)
+        ]
+        picked = [keep.tile([P, S], U32, align_bytes=ALIGN, name=f"picked{a}") for a in range(PASSES)]
+        moving = {}
         raws = {}
-        w8_codes = {}
         gates = {}
 
         def load_table(a):
-            table[a] = shared.tile([P, T], I32, align_bytes=ALIGN, offset=a * TABLE_BYTES, name=f"table{a}")
             nc.sync.dma_start(table[a][:], tab[a, 0:words_bytes].rearrange("(p x) -> p x", p=P).bitcast(I32))
 
-        def load_w4(tile, h, passes):
-            words = w4_words[0:passes, :, h * 2 * HALF : (h + 1) * 2 * HALF]
+        def load_w4_words(tile, h, first, passes):
+            words = w4_words[first : first + passes, :, h * 2 * HALF : (h + 1) * 2 * HALF]
             nc.sync.dma_start(tile[:], words.rearrange("a p x -> p a x").bitcast(I32))
-            for a in range(passes):
-                w4_codes[a, h] = tile[:, a, :]
+            return [tile[:, a, :].bitcast(U8).bitcast(FP4X4) for a in range(passes)]
 
         def load_w4_planes(tile, h, paired_rows):
             nc.vector.memset(tile[:], 0)
-            for r in range(BLOCKS):
-                step = 2 if r >= BLOCKS - paired_rows else 1
+            for r in range(4):
+                step = 2 if r >= 4 - paired_rows else 1
                 for quadrant in range(step):
-                    rows = w4_scales[:, BLOCKS * quadrant + r : 16 : BLOCKS * step, h * HALF : (h + 1) * HALF]
+                    rows = w4_scales[:, 4 * quadrant + r : 16 : 4 * step, h * HALF : (h + 1) * HALF]
                     nc.sync.dma_start(
                         tile[32 * quadrant + r : P : 32 * step, :, :], rows.rearrange("a q n -> q a n").bitcast(I32)
                     )
-            w4_planes[h] = tile[:].rearrange("p a n -> p (a n)").bitcast(U8)
+            flat = tile[:].rearrange("p a n -> p (a n)").bitcast(U8)
+            return [flat[:, a * HALF : (a + 1) * HALF] for a in range(PASSES)]
 
         w4_first = keep.tile([P, LAST, HALF // 2], I32, align_bytes=ALIGN, name="w4_first")
-        load_w4(w4_first, 0, LAST)
+        words_first = load_w4_words(w4_first, 0, 0, LAST)
         scale_rows = shared.tile([P, T // 4], I32, align_bytes=ALIGN, offset=SCALE_ROWS_AT, name="scale_rows")
         nc.sync.dma_start(scale_rows[32:96, :], tab[:, words_bytes:].rearrange("a (q t) -> q a t", q=16).bitcast(I32))
         offsets = keep.tile([P, S // 16], U16, name="offsets")
         nc.sync.dma_start(offsets[:], offs)
         load_table(0)
         planes_first = keep.tile([P, PASSES, HALF // 4], I32, align_bytes=ALIGN, name="planes_first")
-        load_w4_planes(planes_first, 0, PAIRED_ROWS)
+        scales_first = load_w4_planes(planes_first, 0, PAIRED_ROWS)
         load_table(1)
 
         nc.vector.memset(scale_rows[0:32, :], 0)
         nc.vector.memset(scale_rows[96:P, :], 0)
         table_planes = keep.tile([P, PASSES * S // 4], I32, align_bytes=ALIGN, name="table_planes")
         nc.vector.memset(table_planes[:], 0)
-
         picked_scales = keep.tile([P, S], U8, align_bytes=ALIGN, name="picked_scales")
         nc.vector.tensor_copy(picked_scales[:], scale_rows[:].bitcast(U8).indirect(offsets[:]))
-        for low in range(QUADRANTS // 2):
-            for quadrant in (low + 2, low):
-                nc.sync.dma_start(
-                    table_planes[32 * quadrant : 32 * quadrant + BLOCKS, :],
-                    picked_scales[32 + 16 * quadrant : 48 + 16 * quadrant, :].bitcast(I32),
-                )
+        for quadrant in (2, 0, 3, 1):
+            nc.sync.dma_start(
+                table_planes[32 * quadrant : 32 * quadrant + 4, :],
+                picked_scales[32 + 16 * quadrant : 48 + 16 * quadrant, :].bitcast(I32),
+            )
         load_table(2)
         load_table(3)
-        table_planes_u8 = table_planes[:].bitcast(U8)
+        planes = table_planes[:].bitcast(U8)
 
-        picked = [keep.tile([P, S], U32, align_bytes=ALIGN, name=f"picked{a}") for a in range(PASSES)]
-
-        def gather_words(a):
-            n = S // 2 if a == LAST else S
+        def gather(a, parts):
+            n = S // parts
             for first in range(0, S, n):
                 nc.vector.tensor_copy(
                     picked[a][:, first : first + n],
                     table[a][:].bitcast(U32).indirect(offsets[:, first // 16 : (first + n) // 16]),
                 )
-
-        def load_rest_of_w4():
-            w4_last = shared.tile([P, HALF // 2], I32, align_bytes=ALIGN, offset=W4_LAST_AT, name="w4_last")
-            nc.sync.dma_start(w4_last[:], w4_words[LAST, :, 0 : 2 * HALF].bitcast(I32))
-            w4_codes[LAST, 0] = w4_last[:]
-            w4_late = shared.tile([P, PASSES, HALF // 2], I32, align_bytes=ALIGN, offset=W4_LATE_AT, name="w4_late")
-            load_w4(w4_late, 1, PASSES)
-            planes_late = shared.tile(
-                [P, PASSES, HALF // 4], I32, align_bytes=ALIGN, offset=PLANES_LATE_AT, name="planes_late"
-            )
-            load_w4_planes(planes_late, 1, 0)
 
         def load_w8(piece):
             h, a = divmod(piece, PASSES)
@@ -140,16 +115,12 @@ def tile_list_tabglu_tm_none_kernel(tc, tab, w4_words, w4_scales, w8, offs, out)
             rows = w8[512 * a : 512 * (a + 1), h * HALF : (h + 1) * HALF]
             nc.sync.dma_start(raws[a, h][:], rows.rearrange("(p i) n -> p i n", i=4))
 
-        def last_table_under(piece):
-            return min((RAW_AT + (piece + 1) * RAW_BYTES - 1) // TABLE_BYTES, LAST)
-
         def quantize_w8(a, h):
-            if h == 0:
-                cut = 0
-                grouped = stage.tile([P, HALF, 4], BF16, align_bytes=ALIGN, name="grouped")
+            cut = h * SCALAR_COLUMNS // 4
+            if (a, h) == (LAST, 1):
+                grouped = late.tile([P, HALF, 4], BF16, align_bytes=ALIGN, offset=0, name="grouped_last")
             else:
-                cut = SCALAR_COLUMNS // 4
-                grouped = late.tile([P, HALF, 4], BF16, align_bytes=ALIGN, offset=GROUPED_AT[a], name=f"grouped{a}")
+                grouped = keep.tile([P, HALF, 4], BF16, align_bytes=ALIGN, name=f"grouped{a}{h}")
             dst = grouped[:].rearrange("p (c d) i -> p c i d", d=4)
             src = raws[a, h][:].rearrange("p i (c d) -> p c i d", d=4)
             if cut:
@@ -160,83 +131,94 @@ def tile_list_tabglu_tm_none_kernel(tc, tab, w4_words, w4_scales, w8, offs, out)
             nc.vector.quantize_mx(
                 out=codes[:].bitcast(FP8X4), scales=plane[:], in_=grouped[:].rearrange("p n i -> p (n i)")
             )
-            w8_codes[a, h] = (codes, plane)
+            moving["u", a, h] = (codes[:].bitcast(FP8X4), plane[:])
 
         def bank(b, width=HALF):
             return psum.tile([P, width], F32, name=f"bank{b}")
 
-        def multiply(acc, a, t, rhs, rhs_scale):
+        def multiply(acc, product, a, t, h, cols=slice(0, HALF)):
+            words, plane = moving[product, a, h]
             nc.tensor.matmul_mx(
                 out=acc[:],
                 lhsT=picked[a][:, t * P : (t + 1) * P].bitcast(FP8X4),
-                lhsT_scale=table_planes_u8[:, a * S + t * P : a * S + (t + 1) * P],
-                rhs=rhs,
-                rhs_scale=rhs_scale,
+                lhsT_scale=planes[:, a * S + t * P : a * S + (t + 1) * P],
+                rhs=words[:, cols],
+                rhs_scale=plane[:, cols],
                 start=(a == 0),
                 stop=(a == LAST),
             )
-
-        def multiply_w4(acc, a, t, h):
-            multiply(acc, a, t, w4_codes[a, h].bitcast(U8).bitcast(FP4X4), w4_planes[h][:, a * HALF : (a + 1) * HALF])
-
-        def multiply_w8(acc, a, t, h, cols):
-            codes, plane = w8_codes[a, h]
-            multiply(acc, a, t, codes[:, cols].bitcast(FP8X4), plane[:, cols])
 
         def gate(acc, t, h):
             gates[t, h] = keep.tile([P, HALF], F32, align_bytes=ALIGN, name=f"gate{t}{h}")
             nc.scalar.activation(gates[t, h][:], acc[:], SILU)
 
-        def multiply_group(group, h, banks):
-            sums = [(bank(banks[t % len(banks)]), t) for t in group]
-            for a in range(PASSES):
-                for acc, t in sums:
-                    multiply_w8(acc, a, t, h, whole)
-            return sums
-
-        def finish(acc, t, cols):
-            result = keep.tile([P, cols.stop - cols.start], F32, name=f"result{t}_{cols.start}")
-            nc.vector.tensor_tensor(result[:], acc[:], gates[t, 1][:, cols], MULT)
-            queue = nc.sync if t == TOKEN_TILES - 1 else nc.scalar
-            queue.dma_start(out[t * P : (t + 1) * P, HALF + cols.start : HALF + cols.stop], result[:])
-
-        accs = [bank(t) for t in range(TOKEN_TILES)]
+        accs = [bank(t) for t in range(TILES)]
         for a in range(PASSES):
-            gather_words(a)
+            gather(a, 1 if a == 2 else 2)
             if a == 0:
-                load_rest_of_w4()
+                w4_last = shared.tile([P, 1, HALF // 2], I32, align_bytes=ALIGN, offset=W4_LAST_AT, name="w4_last")
+                words_first.extend(load_w4_words(w4_last, 0, LAST, 1))
+                w4_late = shared.tile([P, PASSES, HALF // 2], I32, align_bytes=ALIGN, offset=W4_LATE_AT, name="w4_late")
+                words_late = load_w4_words(w4_late, 1, 0, PASSES)
+                planes_late = shared.tile(
+                    [P, PASSES, HALF // 4], I32, align_bytes=ALIGN, offset=PLANES_LATE_AT, name="planes_late"
+                )
+                scales_late = load_w4_planes(planes_late, 1, 0)
+                for b in range(PASSES):
+                    moving["e", b, 0] = (words_first[b], scales_first[b])
+                    moving["e", b, 1] = (words_late[b], scales_late[b])
             for piece in range(2 * PASSES):
-                if last_table_under(piece) == a:
+                if min((RAW_AT + (piece + 1) * RAW_BYTES - 1) // TABLE_BYTES, LAST) == a:
                     load_w8(piece)
-            for t in range(TOKEN_TILES):
-                multiply_w4(accs[t], a, t, 0)
-        for t in range(TOKEN_TILES):
+            for t in range(TILES):
+                multiply(accs[t], "e", a, t, 0)
+        for t in range(TILES):
             gate(accs[t], t, 0)
 
-        for t in range(TOKEN_TILES):
+        for t in range(TILES):
             if t % 2 == 0:
                 quantize_w8(t // 2, 0)
             acc = bank(t)
-            for turn in range(4 if t == 2 else 1):
-                for a in range(PASSES):
-                    multiply_w4(acc, a, t, 1)
+            for a in range(PASSES):
+                multiply(acc, "e", a, t, 1)
             gate(acc, t, 1)
 
-        for a, group in enumerate(FIRST_HALF_GROUPS):
-            sums = multiply_group(group, 0, range(TOKEN_TILES))
-            quantize_w8(a, 1)
-            results = late.tile([P, len(group), HALF], F32, align_bytes=ALIGN, offset=GROUPED_AT[a], name=f"results{a}")
-            for acc, t in sums:
-                nc.vector.tensor_tensor(results[:, t - group[0], :], acc[:], gates[t, 0][:], MULT)
-            rows = out[group[0] * P : (group[-1] + 1) * P, 0:HALF]
-            nc.sync.dma_start(rows.rearrange("(t p) n -> p t n", p=P), results[:])
+        def sums_of_u(h, tiles):
+            groups = [range(AHEAD)] + [[t] for t in range(AHEAD, tiles)]
+            for group in groups:
+                sums = [(bank(t if h == 0 else SECOND_BANKS[t]), t) for t in group]
+                for a in range(PASSES):
+                    for acc, t in sums:
+                        multiply(acc, "u", a, t, h)
+                for acc, t in sums:
+                    finish(acc, t, h)
 
-        first_parted = LAST_PARTS[0][0]
-        for group in [range(AHEAD)] + [[t] for t in range(AHEAD, first_parted)]:
-            for acc, t in multiply_group(group, 1, SECOND_HALF_BANKS):
-                finish(acc, t, whole)
+        pairs = {}
+
+        def finish(acc, t, h):
+            if h == 0:
+                if t == TILES - 2:
+                    pairs[t // 2] = late.tile([P, 2, HALF], F32, align_bytes=ALIGN, offset=0, name="pair_last")
+                elif t % 2 == 0:
+                    pairs[t // 2] = keep.tile([P, 2, HALF], F32, align_bytes=ALIGN, name=f"pair{t // 2}")
+                nc.vector.tensor_tensor(pairs[t // 2][:, t % 2, :], acc[:], gates[t, 0][:], MULT)
+                if t % 2 == 1:
+                    rows = out[(t - 1) * P : (t + 1) * P, 0:HALF]
+                    nc.sync.dma_start(rows.rearrange("(t p) n -> p t n", p=P), pairs[t // 2][:])
+            else:
+                result = keep.tile([P, HALF], F32, align_bytes=ALIGN, name=f"result{t}")
+                nc.vector.tensor_tensor(result[:], acc[:], gates[t, 1][:], MULT)
+                nc.scalar.dma_start(out[t * P : (t + 1) * P, HALF:M], result[:])
+
+        for a in range(PASSES):
+            quantize_w8(a, 1)
+        sums_of_u(0, TILES)
+        sums_of_u(1, LAST_PARTS[0][0])
         for part, (t, start, stop) in enumerate(LAST_PARTS):
-            acc = bank(SECOND_HALF_BANKS[(first_parted + part) % len(SECOND_HALF_BANKS)], stop - start)
+            acc = bank(SECOND_BANKS[part], stop - start)
             for a in range(PASSES):
-                multiply_w8(acc, a, t, 1, slice(start, stop))
-            finish(acc, t, slice(start, stop))
+                multiply(acc, "u", a, t, 1, slice(start, stop))
+            result = keep.tile([P, stop - start], F32, name=f"part{part}")
+            nc.vector.tensor_tensor(result[:], acc[:], gates[t, 1][:, start:stop], MULT)
+            queue = nc.sync if t == TILES - 1 else nc.scalar
+            queue.dma_start(out[t * P : (t + 1) * P, HALF + start : HALF + stop], result[:])

@@ -29,7 +29,7 @@ W4_LATE_AT = W4_LAST_AT + 2 * HALF
 PLANES_LATE_AT = W4_LATE_AT + PASSES * 2 * HALF
 RAW_AT = PLANES_LATE_AT + PASSES * HALF
 RAW_BYTES = 4 * 4 * HALF
-PAIRED_ROWS = 2
+PAIRED_ROWS = 0
 AHEAD = 4
 SCALAR_COLUMNS = 7 * HALF // 8
 SECOND_BANKS = [0, 1, 2, 3, 6, 7]
@@ -62,13 +62,13 @@ def tile_list_tabglu_tm_none_kernel(tc, tab, w4_words, w4_scales, w8, offs, out)
             nc.sync.dma_start(tile[:], words.rearrange("a p x -> p a x").bitcast(I32))
             return [tile[:, a, :].bitcast(U8).bitcast(FP4X4) for a in range(passes)]
 
-        def load_w4_planes(tile, h, paired_rows):
+        def load_w4_planes(tile, h, paired_rows, queue):
             nc.vector.memset(tile[:], 0)
             for r in range(4):
                 step = 2 if r >= 4 - paired_rows else 1
                 for quadrant in range(step):
                     rows = w4_scales[:, 4 * quadrant + r : 16 : 4 * step, h * HALF : (h + 1) * HALF]
-                    nc.sync.dma_start(
+                    queue.dma_start(
                         tile[32 * quadrant + r : P : 32 * step, :, :], rows.rearrange("a q n -> q a n").bitcast(I32)
                     )
             flat = tile[:].rearrange("p a n -> p (a n)").bitcast(U8)
@@ -82,7 +82,7 @@ def tile_list_tabglu_tm_none_kernel(tc, tab, w4_words, w4_scales, w8, offs, out)
         nc.sync.dma_start(offsets[:], offs)
         load_table(0)
         planes_first = keep.tile([P, PASSES, HALF // 4], I32, align_bytes=ALIGN, name="planes_first")
-        scales_first = load_w4_planes(planes_first, 0, PAIRED_ROWS)
+        scales_first = load_w4_planes(planes_first, 0, PAIRED_ROWS, nc.scalar)
         load_table(1)
 
         nc.vector.memset(scale_rows[0:32, :], 0)
@@ -163,7 +163,7 @@ def tile_list_tabglu_tm_none_kernel(tc, tab, w4_words, w4_scales, w8, offs, out)
                 planes_late = shared.tile(
                     [P, PASSES, HALF // 4], I32, align_bytes=ALIGN, offset=PLANES_LATE_AT, name="planes_late"
                 )
-                scales_late = load_w4_planes(planes_late, 1, 0)
+                scales_late = load_w4_planes(planes_late, 1, 0, nc.sync)
                 for b in range(PASSES):
                     moving["e", b, 0] = (words_first[b], scales_first[b])
                     moving["e", b, 1] = (words_late[b], scales_late[b])

@@ -29,7 +29,7 @@ W4_LATE_AT = W4_LAST_AT + 2 * HALF
 PLANES_LATE_AT = W4_LATE_AT + PASSES * 2 * HALF
 RAW_AT = PLANES_LATE_AT + PASSES * HALF
 RAW_BYTES = 4 * 4 * HALF
-PAIRED_ROWS = 0
+PAIRED_ROWS = 2
 AHEAD = 4
 SCALAR_COLUMNS = 7 * HALF // 8
 SECOND_BANKS = [0, 1, 2, 3, 6, 7]

@@ -63,7 +63,6 @@ def tile_list_tabglu_tm_none_kernel(tc, tab, w4_words, w4_scales, w8, offs, out)
             return [tile[:, a, :].bitcast(U8).bitcast(FP4X4) for a in range(passes)]
 
         def load_w4_planes(tile, h, paired_rows, queue):
-            nc.vector.memset(tile[:], 0)
             for r in range(4):
                 step = 2 if r >= 4 - paired_rows else 1
                 for quadrant in range(step):
@@ -82,6 +81,8 @@ def tile_list_tabglu_tm_none_kernel(tc, tab, w4_words, w4_scales, w8, offs, out)
         nc.sync.dma_start(offsets[:], offs)
         load_table(0)
         planes_first = keep.tile([P, PASSES, HALF // 4], I32, align_bytes=ALIGN, name="planes_first")
+        nc.vector.memset(planes_first[:, 0:2, :], 0)
+        nc.gpsimd.memset(planes_first[:, 2:4, :], 0)
         scales_first = load_w4_planes(planes_first, 0, PAIRED_ROWS, nc.scalar)
         load_table(1)
 
@@ -163,6 +164,7 @@ def tile_list_tabglu_tm_none_kernel(tc, tab, w4_words, w4_scales, w8, offs, out)
                 planes_late = shared.tile(
                     [P, PASSES, HALF // 4], I32, align_bytes=ALIGN, offset=PLANES_LATE_AT, name="planes_late"
                 )
+                nc.vector.memset(planes_late[:], 0)
                 scales_late = load_w4_planes(planes_late, 1, 0, nc.sync)
                 for b in range(PASSES):
                     moving["e", b, 0] = (words_first[b], scales_first[b])

@@ -155,7 +155,7 @@ def tile_list_tabglu_tm_none_kernel(tc, tab, w4_words, w4_scales, w8, offs, out)
 
         accs = [bank(t) for t in range(TILES)]
         for a in range(PASSES):
-            gather(a, 1 if a == 2 else 2)
+            gather(a, 4 if a == LAST else 1)
             if a == 0:
                 w4_last = shared.tile([P, 1, HALF // 2], I32, align_bytes=ALIGN, offset=W4_LAST_AT, name="w4_last")
                 words_first.extend(load_w4_words(w4_last, 0, LAST, 1))

@@ -31,6 +31,7 @@ RAW_AT = PLANES_LATE_AT + PASSES * HALF
 RAW_BYTES = 4 * 4 * HALF
 PAIRED_ROWS = 2
 AHEAD = 4
+GATHER_CUTS = [[0, S], [0, 3 * P, S], [0, 3 * P, S], [0, 2 * P, 4 * P, 6 * P, S]]
 SCALAR_COLUMNS = 7 * HALF // 8
 SECOND_BANKS = [0, 1, 2, 3, 6, 7]
 LAST_PARTS = [(6, 0, 256), (6, 256, 512), (7, 0, 256), (7, 256, 384), (7, 384, 512)]
@@ -101,12 +102,11 @@ def tile_list_tabglu_tm_none_kernel(tc, tab, w4_words, w4_scales, w8, offs, out)
         load_table(3)
         planes = table_planes[:].bitcast(U8)
 
-        def gather(a, parts):
-            n = S // parts
-            for first in range(0, S, n):
+        def gather(a):
+            for first, stop in zip(GATHER_CUTS[a], GATHER_CUTS[a][1:]):
                 nc.vector.tensor_copy(
-                    picked[a][:, first : first + n],
-                    table[a][:].bitcast(U32).indirect(offsets[:, first // 16 : (first + n) // 16]),
+                    picked[a][:, first:stop],
+                    table[a][:].bitcast(U32).indirect(offsets[:, first // 16 : stop // 16]),
                 )
 
         def load_w8(piece):
@@ -155,7 +155,7 @@ def tile_list_tabglu_tm_none_kernel(tc, tab, w4_words, w4_scales, w8, offs, out)
 
         accs = [bank(t) for t in range(TILES)]
         for a in range(PASSES):
-            gather(a, 4 if a == LAST else 1)
+            gather(a)
             if a == 0:
                 w4_last = shared.tile([P, 1, HALF // 2], I32, align_bytes=ALIGN, offset=W4_LAST_AT, name="w4_last")
                 words_first.extend(load_w4_words(w4_last, 0, LAST, 1))

@@ -215,7 +215,23 @@ def tile_list_tabglu_tm_none_kernel(tc, tab, w4_words, w4_scales, w8, offs, out)
         for a in range(PASSES):
             quantize_w8(a, 1)
         sums_of_u(0, TILES)
-        sums_of_u(1, LAST_PARTS[0][0])
+        sums = [bank(SECOND_BANKS[t]) for t in range(AHEAD + 1)]
+        for a in range(LAST):
+            for t in range(AHEAD):
+                multiply(sums[t], "u", a, t, 1)
+        multiply(sums[AHEAD], "u", 0, AHEAD, 1)
+        for t in range(AHEAD):
+            multiply(sums[t], "u", LAST, t, 1)
+        for t in range(AHEAD):
+            finish(sums[t], t, 1)
+        for a in range(1, PASSES):
+            multiply(sums[AHEAD], "u", a, AHEAD, 1)
+        finish(sums[AHEAD], AHEAD, 1)
+        for t in range(AHEAD + 1, LAST_PARTS[0][0]):
+            acc = bank(SECOND_BANKS[t])
+            for a in range(PASSES):
+                multiply(acc, "u", a, t, 1)
+            finish(acc, t, 1)
         for part, (t, start, stop) in enumerate(LAST_PARTS):
             acc = bank(SECOND_BANKS[part], stop - start)
             for a in range(PASSES):

from contextlib import ExitStack

import concourse.mybir as mybir

K, M, T, S = 2048, 1024, 4096, 1024
FLOPS = 2 * 2 * K * M * S

F32 = mybir.dt.float32
BF16 = mybir.dt.bfloat16
I32 = mybir.dt.int32
U32 = mybir.dt.uint32
U16 = mybir.dt.uint16
U8 = mybir.dt.uint8
FP8X4 = mybir.dt.float8_e4m3fn_x4
FP4X4 = mybir.dt.float4_e2m1fn_x4
SILU = mybir.ActivationFunctionType.Silu
MULT = mybir.AluOpType.mult

P = 128
PASSES = K // 512
LAST = PASSES - 1
HALF = M // 2
TILES = S // P
ALIGN = 256
TABLE_BYTES = 4 * T
SCALE_ROWS_AT = 3 * TABLE_BYTES - T // 2
W4_LAST_AT = 0
W4_LATE_AT = W4_LAST_AT + 2 * HALF
PLANES_LATE_AT = W4_LATE_AT + PASSES * 2 * HALF
RAW_AT = PLANES_LATE_AT + PASSES * HALF
RAW_BYTES = 4 * 4 * HALF
PAIRED_ROWS = 2
AHEAD = 4
GATHER_CUTS = [[0, S], [0, 3 * P, S], [0, 3 * P, S], [0, 2 * P, 4 * P, 6 * P, S]]
SCALAR_COLUMNS = 7 * HALF // 8
SECOND_BANKS = [0, 1, 2, 3, 6, 7]
LAST_PARTS = [(6, 0, 256), (6, 256, 512), (7, 0, 256), (7, 256, 384), (7, 384, 512)]


def tile_list_tabglu_tm_none_kernel(tc, tab, w4_words, w4_scales, w8, offs, out):
    nc = tc.nc
    words_bytes = P * TABLE_BYTES

    with ExitStack() as ctx:
        keep = ctx.enter_context(tc.tile_pool(name="keep", bufs=1))
        shared = ctx.enter_context(tc.tile_pool(name="shared", bufs=1))
        late = ctx.enter_context(tc.tile_pool(name="late", bufs=1))
        psum = ctx.enter_context(tc.psum_pool(name="psum", bufs=1))

        table = [
            shared.tile([P, T], I32, align_bytes=ALIGN, offset=a * TABLE_BYTES, name=f"table{a}") for a in range(PASSES)
        ]
        picked = [keep.tile([P, S], U32, align_bytes=ALIGN, name=f"picked{a}") for a in range(PASSES)]
        moving = {}
        raws = {}
        gates = {}

        def load_table(a):
            nc.sync.dma_start(table[a][:], tab[a, 0:words_bytes].rearrange("(p x) -> p x", p=P).bitcast(I32))

        def load_w4_words(tile, h, first, passes):
            words = w4_words[first : first + passes, :, h * 2 * HALF : (h + 1) * 2 * HALF]
            nc.sync.dma_start(tile[:], words.rearrange("a p x -> p a x").bitcast(I32))
            return [tile[:, a, :].bitcast(U8).bitcast(FP4X4) for a in range(passes)]

        def load_w4_planes(tile, h, paired_rows, queue):
            for r in range(4):
                step = 2 if r >= 4 - paired_rows else 1
                for quadrant in range(step):
                    rows = w4_scales[:, 4 * quadrant + r : 16 : 4 * step, h * HALF : (h + 1) * HALF]
                    queue.dma_start(
                        tile[32 * quadrant + r : P : 32 * step, :, :], rows.rearrange("a q n -> q a n").bitcast(I32)
                    )
            flat = tile[:].rearrange("p a n -> p (a n)").bitcast(U8)
            return [flat[:, a * HALF : (a + 1) * HALF] for a in range(PASSES)]

        w4_first = keep.tile([P, LAST, HALF // 2], I32, align_bytes=ALIGN, name="w4_first")
        words_first = load_w4_words(w4_first, 0, 0, LAST)
        scale_rows = shared.tile([P, T // 4], I32, align_bytes=ALIGN, offset=SCALE_ROWS_AT, name="scale_rows")
        nc.sync.dma_start(scale_rows[32:96, :], tab[:, words_bytes:].rearrange("a (q t) -> q a t", q=16).bitcast(I32))
        offsets = keep.tile([P, S // 16], U16, name="offsets")
        nc.sync.dma_start(offsets[:], offs)
        load_table(0)
        planes_first = keep.tile([P, PASSES, HALF // 4], I32, align_bytes=ALIGN, name="planes_first")
        nc.vector.memset(planes_first[:, 0:2, :], 0)
        nc.gpsimd.memset(planes_first[:, 2:4, :], 0)
        scales_first = load_w4_planes(planes_first, 0, PAIRED_ROWS, nc.scalar)
        load_table(1)

        nc.vector.memset(scale_rows[0:32, :], 0)
        nc.vector.memset(scale_rows[96:P, :], 0)
        table_planes = keep.tile([P, PASSES * S // 4], I32, align_bytes=ALIGN, name="table_planes")
        nc.vector.memset(table_planes[:], 0)
        picked_scales = keep.tile([P, S], U8, align_bytes=ALIGN, name="picked_scales")
        nc.vector.tensor_copy(picked_scales[:], scale_rows[:].bitcast(U8).indirect(offsets[:]))
        for quadrant in (2, 0, 3, 1):
            nc.sync.dma_start(
                table_planes[32 * quadrant : 32 * quadrant + 4, :],
                picked_scales[32 + 16 * quadrant : 48 + 16 * quadrant, :].bitcast(I32),
            )
        load_table(2)
        load_table(3)
        planes = table_planes[:].bitcast(U8)

        def gather(a):
            for first, stop in zip(GATHER_CUTS[a], GATHER_CUTS[a][1:]):
                nc.vector.tensor_copy(
                    picked[a][:, first:stop],
                    table[a][:].bitcast(U32).indirect(offsets[:, first // 16 : stop // 16]),
                )

        def load_w8(piece):
            h, a = divmod(piece, PASSES)
            at = RAW_AT + piece * RAW_BYTES
            raws[a, h] = shared.tile([P, 4, HALF], F32, align_bytes=ALIGN, offset=at, name=f"raw{a}{h}")
            rows = w8[512 * a : 512 * (a + 1), h * HALF : (h + 1) * HALF]
            nc.sync.dma_start(raws[a, h][:], rows.rearrange("(p i) n -> p i n", i=4))

        def quantize_w8(a, h):
            cut = h * SCALAR_COLUMNS // 4
            if (a, h) == (LAST, 1):
                grouped = late.tile([P, HALF, 4], BF16, align_bytes=ALIGN, offset=0, name="grouped_last")
            else:
                grouped = keep.tile([P, HALF, 4], BF16, align_bytes=ALIGN, name=f"grouped{a}{h}")
            dst = grouped[:].rearrange("p (c d) i -> p c i d", d=4)
            src = raws[a, h][:].rearrange("p i (c d) -> p c i d", d=4)
            if cut:
                nc.scalar.copy(dst[:, :cut], src[:, :cut])
            nc.vector.tensor_copy(dst[:, cut:], src[:, cut:])
            codes = keep.tile([P, HALF], U32, align_bytes=ALIGN, name=f"w8_codes{a}{h}")
            plane = keep.tile([P, HALF], U8, align_bytes=ALIGN, name=f"w8_plane{a}{h}")
            nc.vector.quantize_mx(
                out=codes[:].bitcast(FP8X4), scales=plane[:], in_=grouped[:].rearrange("p n i -> p (n i)")
            )
            moving["u", a, h] = (codes[:].bitcast(FP8X4), plane[:])

        def bank(b, width=HALF):
            return psum.tile([P, width], F32, name=f"bank{b}")

        def multiply(acc, product, a, t, h, cols=slice(0, HALF)):
            words, plane = moving[product, a, h]
            nc.tensor.matmul_mx(
                out=acc[:],
                lhsT=picked[a][:, t * P : (t + 1) * P].bitcast(FP8X4),
                lhsT_scale=planes[:, a * S + t * P : a * S + (t + 1) * P],
                rhs=words[:, cols],
                rhs_scale=plane[:, cols],
                start=(a == 0),
                stop=(a == LAST),
            )

        def gate(acc, t, h):
            gates[t, h] = keep.tile([P, HALF], F32, align_bytes=ALIGN, name=f"gate{t}{h}")
            nc.scalar.activation(gates[t, h][:], acc[:], SILU)

        accs = [bank(t) for t in range(TILES)]
        for a in range(PASSES):
            gather(a)
            if a == 0:
                w4_last = shared.tile([P, 1, HALF // 2], I32, align_bytes=ALIGN, offset=W4_LAST_AT, name="w4_last")
                words_first.extend(load_w4_words(w4_last, 0, LAST, 1))
                w4_late = shared.tile([P, PASSES, HALF // 2], I32, align_bytes=ALIGN, offset=W4_LATE_AT, name="w4_late")
                words_late = load_w4_words(w4_late, 1, 0, PASSES)
                planes_late = shared.tile(
                    [P, PASSES, HALF // 4], I32, align_bytes=ALIGN, offset=PLANES_LATE_AT, name="planes_late"
                )
                nc.vector.memset(planes_late[:], 0)
                scales_late = load_w4_planes(planes_late, 1, 0, nc.sync)
                for b in range(PASSES):
                    moving["e", b, 0] = (words_first[b], scales_first[b])
                    moving["e", b, 1] = (words_late[b], scales_late[b])
            for piece in range(2 * PASSES):
                if min((RAW_AT + (piece + 1) * RAW_BYTES - 1) // TABLE_BYTES, LAST) == a:
                    load_w8(piece)
            for t in range(TILES):
                multiply(accs[t], "e", a, t, 0)
        for t in range(TILES):
            gate(accs[t], t, 0)

        for t in range(TILES):
            if t % 2 == 0:
                quantize_w8(t // 2, 0)
            acc = bank(t)
            for a in range(PASSES):
                multiply(acc, "e", a, t, 1)
            gate(acc, t, 1)

        def sums_of_u(h, tiles):
            groups = [range(AHEAD)] + [[t] for t in range(AHEAD, tiles)]
            for group in groups:
                sums = [(bank(t if h == 0 else SECOND_BANKS[t]), t) for t in group]
                for a in range(PASSES):
                    for acc, t in sums:
                        multiply(acc, "u", a, t, h)
                for acc, t in sums:
                    finish(acc, t, h)

        pairs = {}

        def finish(acc, t, h):
            if h == 0:
                if t == TILES - 2:
                    pairs[t // 2] = late.tile([P, 2, HALF], F32, align_bytes=ALIGN, offset=0, name="pair_last")
                elif t % 2 == 0:
                    pairs[t // 2] = keep.tile([P, 2, HALF], F32, align_bytes=ALIGN, name=f"pair{t // 2}")
                nc.vector.tensor_tensor(pairs[t // 2][:, t % 2, :], acc[:], gates[t, 0][:], MULT)
                if t % 2 == 1:
                    rows = out[(t - 1) * P : (t + 1) * P, 0:HALF]
                    nc.sync.dma_start(rows.rearrange("(t p) n -> p t n", p=P), pairs[t // 2][:])
            else:
                result = keep.tile([P, HALF], F32, align_bytes=ALIGN, name=f"result{t}")
                nc.vector.tensor_tensor(result[:], acc[:], gates[t, 1][:], MULT)
                nc.scalar.dma_start(out[t * P : (t + 1) * P, HALF:M], result[:])

        for a in range(PASSES):
            quantize_w8(a, 1)
        sums_of_u(0, TILES)
        sums = [bank(SECOND_BANKS[t]) for t in range(AHEAD + 1)]
        for a in range(LAST):
            for t in range(AHEAD):
                multiply(sums[t], "u", a, t, 1)
        multiply(sums[AHEAD], "u", 0, AHEAD, 1)
        for t in range(AHEAD):
            multiply(sums[t], "u", LAST, t, 1)
        for t in range(AHEAD):
            finish(sums[t], t, 1)
        for a in range(1, PASSES):
            multiply(sums[AHEAD], "u", a, AHEAD, 1)
        finish(sums[AHEAD], AHEAD, 1)
        for t in range(AHEAD + 1, LAST_PARTS[0][0]):
            acc = bank(SECOND_BANKS[t])
            for a in range(PASSES):
                multiply(acc, "u", a, t, 1)
            finish(acc, t, 1)
        for part, (t, start, stop) in enumerate(LAST_PARTS):
            acc = bank(SECOND_BANKS[part], stop - start)
            for a in range(PASSES):
                multiply(acc, "u", a, t, 1, slice(start, stop))
            result = keep.tile([P, stop - start], F32, name=f"part{part}")
            nc.vector.tensor_tensor(result[:], acc[:], gates[t, 1][:, start:stop], MULT)
            queue = nc.sync if t == TILES - 1 else nc.scalar
            queue.dma_start(out[t * P : (t + 1) * P, HALF + start : HALF + stop], result[:])
